import numpy as np, ml_dtypes
CORES = [36,164,52,180,100,228,116,244]
N = 8
import mx_ref
BF = ml_dtypes.bfloat16
def cols(t, e):
    v = np.concatenate([t.reshape(128, -1, 4), np.zeros((128, 1, 4), BF)], axis=1)
    return np.ascontiguousarray(v[:, e]).reshape(128, -1)
def cut(t, i, w=512):
    return t[:, w * i:w * i + w]
def pick(q, e):
    c = np.concatenate([q[0].reshape(128, -1, 4), np.zeros((128, 1, 4), np.uint8)], axis=1); s = np.concatenate([q[1], np.ones((16, 1), np.uint8)], axis=1)
    return (np.ascontiguousarray(c[:, e].reshape(128, -1)), np.ascontiguousarray(s[:, e]))
def join(*qs):
    return (np.concatenate([q[0] for q in qs], axis=1), np.concatenate([q[1] for q in qs], axis=1))
def put(q, e, v):
    c, s = q[0].reshape(128, -1, 4).copy(), q[1].copy(); c[:, e] = v[0].reshape(128, -1, 4); s[:, e] = v[1]
    return (c.reshape(128, -1), s)
def pk(c, s):
    return (np.ascontiguousarray(c), mx_ref.live(s))
def emit(q):
    return q[0], q[1]
def decode(q):
    o = []
    for b in range(4):
        e = np.zeros((128, 128, 4), np.float32); e[np.arange(128), np.arange(128), b] = 1
        o.append(mx_ref.matmul(mx_ref.quantize(e.reshape(128, 512).astype(BF)), q))
    return np.stack(o, axis=2).reshape(128, -1)
def f(rng, *shape):
    return mx_ref.flush((rng.standard_normal(shape, dtype=np.float32) * np.exp2(rng.integers(-2, 3, shape[:-1] + (1,)))).astype(BF))
def wide(rng, *shape, cols=0):
    v = rng.standard_normal(shape, dtype=np.float32) * np.exp2(rng.integers(-12, 13, shape)).astype(np.float32)
    if cols: v *= np.repeat(np.exp2(rng.integers(-cols, cols + 1, shape[:-2] + (1, shape[-1] // 4))) * (rng.random(shape[:-2] + (1, shape[-1] // 4)) > 0.0625), 4, axis=-1).astype(np.float32)
    return mx_ref.flush(v.astype(BF))
P, K, R, O = 128, 16, 2, 1
def big(v):
    v = v.astype(np.float32)
    v[np.abs(v) < np.float32(2.0 ** -16)] = 0
    return v.astype(BF)
def times(t, k):
    return mx_ref.flush((t.astype(np.float32) * np.float32(k)).astype(BF))
def signs(d, v, s):
    g = np.where(d["u"][0, :, :4].astype(np.float32) < 0, -1, 1)
    a = np.abs(v.astype(np.float32)).reshape(N, 128, -1, 4) * g[None, :, None, :] * s[:, None, :, None]
    return big(a.reshape(N, 128, -1))
def counted(rng, d):
    n = P // 2 + rng.permutation(K)[:N]
    return signs(d, d["tb"], np.stack([np.where(rng.permutation(P) < n[r], 1, -1) for r in range(N)]))
def setup_inputs(rng):
    v = np.zeros((128, 512), np.float32)
    v[:, :4] = f(rng, 128, 4).astype(np.float32)
    return {"tb": big(f(rng, N, 128, 4 * P)), "nz": big(f(rng, N, 128, 4 * R * K)), "u": np.stack([v.astype(BF)] * N), "w": f(rng, N, 128, 512 * O)}
def setup_inputs_down(rng):
    d = setup_inputs(rng)
    d["tb"] = counted(rng, d)
    d["nz"] = signs(d, 64 * (1 + rng.random((N, 128, 4 * R * K))), np.full((N, R * K), -1))
    return d
def setup_inputs_spread(rng):
    d = setup_inputs(rng)
    t, r = big(wide(rng, N, 128, 4 * P, cols=6)), int(rng.integers(0, N))
    x = (1 + rng.random((N, 128, 4 * P))) * np.exp2(rng.integers(12, 18, (N, 128, 4 * P)) + np.repeat(rng.integers(0, 4, (N, 1, P)), 4, axis=2))
    t[r] = signs(d, x, np.ones((N, P), np.int64))[r]
    return {**d, "tb": t, "nz": big(wide(rng, N, 128, 4 * R * K, cols=6)), "u": times(d["u"], 2.0 ** 24)}
def setup_inputs_swap(rng):
    d = setup_inputs(rng)
    d["tb"] = counted(rng, d)
    d["nz"] = signs(d, 64 * (1 + rng.random((N, 128, 4 * R * K))), np.full((N, R * K), 1))
    return d
def setup_inputs_ties(rng):
    d = setup_inputs(rng)
    a = rng.permutation(N) <= N // 2
    d["tb"] = np.stack([cols(d["tb"][int(a[r])], rng.permutation(P) % (P // (K + 1))) for r in range(N)])
    d["nz"] = np.stack([d["nz"][0]] * N)
    return d
def setup_inputs_zero(rng):
    d = setup_inputs(rng)
    d["u"] = times(np.abs(d["u"].astype(np.float32)), 2.0 ** -26)
    d["tb"], d["nz"] = big(times(d["tb"], 2.0 ** -10)), big(times(d["nz"], 2.0 ** -10))
    s, a = np.zeros((N, P), np.int64), rng.permutation(N)
    for i in range(N - 1):
        m, n, e = P // 2 - 4 * i, K // 2 - i, rng.permutation(P)
        s[a[i], e[:m]] = 1
        s[a[i], e[m:m + n]] = -1
    d["tb"] = signs(d, d["tb"], s)
    for r in range(N):
        d["tb"][r].reshape(128, P, 4)[:, np.flatnonzero(s[r] == 0)[1::2]] = BF(-0.0)
    d["nz"] = big(d["nz"].astype(np.float32) * np.repeat(rng.random((N, 1, R * K)) > 0.25, 4, axis=2))
    return d
def check_inputs(d):
    b = []
    for k, low, high in (("tb", -16, 26), ("nz", -16, 26), ("u", -30, 30), ("w", -30, 30)):
        v = np.abs(d[k].astype(np.float32))
        if not (np.isfinite(v).all() and ((v == 0) | (v >= 2.0 ** low) & (v <= 2.0 ** high)).all()): b.append("a value of " + k)
    v = d["u"].astype(np.float32)
    if (v[:, :, 4:] != 0).any(): b.append("u has numbers behind its column 0")
    if (v != v[:1]).any(): b.append("u isn't the same on all ranks")
    return b
def reference(tb, nz, u, w):
    T = [mx_ref.quantize(tb[r]) for r in range(N)]
    qu = [mx_ref.quantize(u[r]) for r in range(N)]
    od = np.zeros((N, R, N), np.float32)
    for t in range(R):
        s = [mx_ref.matmul(qu[r], T[r])[0] + np.float32(0) for r in range(N)]
        fitness = np.array([np.count_nonzero(s[r] > 0) for r in range(N)])
        place = np.argsort(-fitness, kind="stable")
        od[:, t] = place
        new = T[:]
        for i in range(N // 2):
            a, b = place[i], place[N - 1 - i]
            j = np.argsort(s[a], kind="stable")[:K]
            noise = mx_ref.quantize(np.ascontiguousarray(nz[b][:, 4 * t * K:4 * (t + 1) * K]))
            v = np.float32(0.5) * decode(pick(T[a], j)) + np.float32(0.5) * decode(noise)
            new[b] = put(T[a], j, mx_ref.quantize(np.ascontiguousarray(v.astype(BF))))
        T = new
    oc, osc, y = np.zeros((N, 128, 4 * P), np.uint8), np.zeros((N, 16, P), np.uint8), np.zeros((N, 128, O * P), np.float32)
    for r in range(N):
        oc[r], osc[r] = emit(T[r])
        for o in range(O):
            y[r, :, o * P:(o + 1) * P] = mx_ref.matmul(mx_ref.quantize(np.ascontiguousarray(cut(w[r], o))), T[r])
    return {"oc": oc, "osc": osc, "od": od, "y": y}

@@ -1,0 +1,548 @@
+from concourse.bass import DstId, RemoteDMATransfer
+from concourse.mybir import dt, AluOpType, AxisListType, ActivationFunctionType
+
+A = AluOpType
+F = ActivationFunctionType
+NR, SL = 8, 18
+ROWS = ["KR", "KT", "REP", "PR", "REPB", "BR0", "REPF", "FBR", "KR1", "KT1", "RE1", "PR1", "RE2", "FR", "RO0", "OD0", "RO1", "OD1"]
+TINY, BIG = 2.0 ** -100, 1e29
+
+_f, _b, _u = "float32", "bfloat16", "uint16"
+
+
+def _mx(d, name, n):
+    d[name] = ("sbuf", [128, n], "float8_e4m3fn_x4")
+    d[name + "s"] = ("sbuf", [128, n], "uint8")
+
+
+SCRATCH = {}
+for _n, _w, _t in (
+        ("TB", 512, _b), ("UC", 4, _b), ("NUC", 4, _b), ("NZ", 128, _b), ("WT", 512, _b), ("ZB", 576, _b), ("UT", 512, _b), ("NU", 512, _b),
+        ("CI", 8, "int32"), ("CF", 8, _f), ("CK", 16, _f), ("J32", 32, _f), ("KI", 128, _b), ("IREF", 128, _b), ("OH2", 256, _b),
+        ("OHREF", 512, _b), ("QR", 128, _b), ("HALF", 520, _b), ("ZE", 520, _b), ("TIE", 128, _f), ("DIAG", 128, _f), ("RM", 128, _f),
+        ("M32", 32, _f), ("MS", 8, _f), ("JC", 8, _f), ("TIE8", 8, _f), ("W8", 8, _f), ("Z32", 32, _f),
+        ("MVC", 512, _b), ("ONE", 512, _b), ("ZW", 512, _b), ("ST4", 512, _b), ("NT0", 576, _b), ("NT1", 576, _b),
+        ("INFO", 512, _b), ("OHT", 512, _b), ("CMP", 128, _f), ("SM", 384, _f), ("R32", 32 * len(ROWS), _f),
+        ("V0", 576, _b), ("V1", 576, _b), ("NZ1", 80, _f), ("TH8", 8, _f), ("THR", 128, _f), ("ZT", 512, _b),
+        ("DD", 128, _f), ("SQ", 128, _f), ("TI1", 128, _f), ("TA", 128, _f), ("IND", 128, _f), ("CS", 128, _f),
+        ("D5", 512, _f), ("MT", 512, _b), ("VT", 512, _b), ("OHL", 128, _b), ("STT", 512, _b), ("NT", 512, _b), ("Y", 128, _f), ("CM1", 128, _f),
+        ("OFF1", 4, _u), ("OFFH", 2, _u), ("OFF3", 8, _u), ("OFFO", 2, _u), ("OFFG", 32, _u), ("OFFF", 8, _u), ("OFT", 8, _u)):
+    SCRATCH[_n] = ("sbuf", [128, _w], _t)
+for _n, _w in (("UQ", 128), ("NUQ", 128), ("TQ", 128), ("MVQ", 128), ("OHQ", 128), ("ONQ", 128), ("EQ", 512), ("N0Q", 144), ("N1Q", 144),
+               ("WQ", 128), ("ZWQ", 128), ("S4Q", 128), ("L1S", 144), ("LD1", 144), ("NB", 160), ("W2", 528), ("PH1", 128), ("S3", 128),
+               ("ZQ", 128), ("MQ", 128), ("STQ", 128), ("NTQ", 128), ("FT", 128), ("HT", 128)):
+    _mx(SCRATCH, _n, _w)
+for _n, _w in (("PV", 2048), ("PA", 512), ("PB", 512), ("PC", 512), ("PD", 512)):
+    SCRATCH[_n] = ("psum", [128, _w], _f)
+
+SEMAPHORES = ["sv", "sa", "st", "sg", "arrh", "arr1", "arr2", "arr3", "arrp"]
+SEMAPHORES += ["d%d" % i for i in range(24)] + ["l%d" % i for i in range(12)]
+
+
+def _helper_of(topo, core):
+    return [c for c in topo.cores_of(core) if topo.die(c) != topo.die(core)][0]
+
+
+def _dst(topo, d, s):
+    rid, pid = topo.addr(d, s)
+    return DstId(rid=rid, pnc=pid)
+
+
+def _hand_on(g, core, T, topo, owner):
+    me = T.rank_of(owner)
+    g.wait_ge(T.sem.arrh, 2 * len(topo.engines(owner, core)))
+    for k, (src, dst) in enumerate((("HT", "PH1"), ("HTs", "PH1s"))):
+        tr = []
+        for i, d in enumerate(x for x in range(NR) if x != me):
+            c = T.cores[d]
+            s, t = T[src][:, 16 * d:16 * d + 16], T[dst][:, 16 * me:16 * me + 16]
+            if k == 0:
+                s, t = s.bitcast(dt.uint8), t.bitcast(dt.uint8)
+            tr.append(RemoteDMATransfer(dst_ids=[_dst(topo, c, core)], dma_engine_mask=1 << topo.engines(core, c)[i],
+                                        remote_sem=T.sem.arrp, srcs=[s], dsts=[t]))
+        g.remote_dma_fused(tr, local_sem=T.sem["l%d" % k])
+    for k in range(2):
+        g.wait_ge(T.sem["l%d" % k], NR - 1)
+
+
+def rank_program(g, core, T, topo):
+    me = T.rank_of(core)
+    if me is None:
+        for c in T.cores:
+            if _helper_of(topo, c) == core:
+                _hand_on(g, core, T, topo, c)
+        return
+    ENG = {"v": g.vector, "a": g.scalar, "t": g.tensor, "g": g, "s": g.sync}
+    SEM = {"v": "sv", "a": "sa", "t": "st", "g": "sg"}
+    cnt, seen, acc, nd, nl, ends = {}, {q: {} for q in ENG}, {}, [0], [0], []
+
+    def clash(a, lo, hi, st):
+        if a[1] <= lo or hi <= a[0]:
+            return False
+        return not (a[2] == st and st > 1 and a[0] % st != lo % st)
+
+    def span(x):
+        if SCRATCH[x[0]][0] == "psum":
+            return x[0], x[1] // 512 * 512, (x[2] + 511) // 512 * 512, 1
+        return x[0], x[1], x[2], x[3]
+
+    def waits(q, rd, wr, dma=False):
+        need = {}
+        for w, xs in ((False, rd), (True, wr)):
+            for x in xs:
+                if x[0] not in SCRATCH:
+                    continue
+                n, lo, hi, st = span(x)
+                ps = SCRATCH[n][0] == "psum"
+                for a in acc.get(n, []):
+                    if not clash(a, lo, hi, st):
+                        continue
+                    same = a[4] == q and not dma and not a[6]
+                    if same and (q == "t" or not a[3]):
+                        continue
+                    if not (w or a[3]) and (same or not ps):
+                        continue
+                    need[a[5][0]] = max(need.get(a[5][0], 0), a[5][1])
+        for s, val in need.items():
+            if seen[q].get(s, 0) < val:
+                ENG[q].wait_ge(T.sem[s], val)
+                seen[q][s] = val
+
+    def note(q, rd, wr, tok, dma=False):
+        for w, xs in ((False, rd), (True, wr)):
+            for x in xs:
+                if x[0] in SCRATCH:
+                    n, lo, hi, st = span(x)
+                    acc.setdefault(n, []).append((lo, hi, st, w, q, tok, dma))
+
+    def v(n, lo=0, hi=None, st=1):
+        if n in ROWS:
+            o = 32 * ROWS.index(n)
+            return ("R32", o + lo, o + (32 if hi is None else hi), st)
+        return (n, lo, SCRATCH[n][1][1] if hi is None else hi, st)
+
+    def ap(x):
+        return T[x[0]][:, x[1]:x[2]] if x[3] == 1 else T[x[0]][:, x[1]:x[2]:x[3]]
+
+    def op(q, fn, rd, wr):
+        waits(q, rd, wr)
+        cnt[q] = cnt.get(q, 0) + 1
+        fn().then_inc(T.sem[SEM[q]], 1)
+        note(q, rd, wr, (SEM[q], cnt[q]))
+
+    def sc(x):
+        return ap(x) if isinstance(x, tuple) else x
+
+    def ts(out, in0, s1, op0, s2=None, op1=None):
+        rd = [in0] + [s for s in (s1, s2) if isinstance(s, tuple)]
+        if op1 is None:
+            op("v", lambda: g.vector.tensor_scalar(ap(out), ap(in0), sc(s1), None, op0), rd, [out])
+        else:
+            op("v", lambda: g.vector.tensor_scalar(ap(out), ap(in0), sc(s1), sc(s2), op0, op1), rd, [out])
+
+    def tt(out, a, b, o):
+        op("v", lambda: g.vector.tensor_tensor(ap(out), ap(a), ap(b), o), [a, b], [out])
+
+    def red(out, a):
+        op("v", lambda: g.vector.tensor_reduce(ap(out), ap(a), AxisListType.X, A.add), [a], [out])
+
+    def cp(out, a):
+        op("v", lambda: g.vector.tensor_copy(ap(out), ap(a)), [a], [out])
+
+    def tr(out, a):
+        op("v", lambda: g.vector.transpose(ap(out), ap(a)), [a], [out])
+
+    def ms(out, c):
+        op("v", lambda: g.vector.memset(ap(out), c), [], [out])
+
+    def act(out, a, fn=F.Copy, **kw):
+        k2 = {k: sc(x) for k, x in kw.items()}
+        op("a", lambda: g.scalar.activation(ap(out), ap(a), fn, **k2), [a] + [x for x in kw.values() if isinstance(x, tuple)], [out])
+
+    def quant(out, in_):
+        o2 = v(out[0] + "s", out[1], out[2])
+        op("v", lambda: g.vector.quantize_mx(ap(out), ap(o2), ap(in_)), [in_], [out, o2])
+
+    def mm(out, w, x, start=True, stop=True):
+        ws, xs = v(w[0] + "s", w[1], w[2]), v(x[0] + "s", x[1], x[2])
+        op("t", lambda: g.tensor.matmul_mx(ap(out), ap(w), ap(ws), ap(x), ap(xs), start, stop), [w, ws, x, xs], [out])
+
+    def pick_c(out, win, off):
+        op("v", lambda: g.vector.tensor_copy(ap(out).bitcast(dt.uint32), ap(win).bitcast(dt.uint32).indirect(ap(off))), [win, off], [out])
+
+    def pick_s(out, win, off):
+        out, win = v(out[0] + "s", out[1], out[2]), v(win[0] + "s", win[1], win[2])
+        op("a", lambda: g.scalar.activation(ap(out), ap(win).indirect(ap(off)), F.Copy), [win, off], [out])
+
+    def dma(q, out, in_, oap=None, iap=None):
+        waits(q, [in_], [out], True)
+        s = "d%d" % nd[0]
+        nd[0] += 1
+        ENG[q].dma_start(ap(out) if oap is None else oap, ap(in_) if iap is None else iap).then_inc(T.sem[s], 16)
+        note(q, [in_], [out], (s, 16), True)
+        ends.append((s, 16))
+
+    def codes(x):
+        return ap(x).bitcast(dt.uint8)
+
+    def landed(n, lo, hi, tok):
+        if hi > lo:
+            for m in (n, n + "s"):
+                note("-", [], [v(m, lo, hi)], tok, True)
+
+    def send(x, transfers):
+        waits("g", [t[2] for t in transfers], [], True)
+        s, n = "l%d" % nl[0], 0
+        nl[0] += 1
+        out = []
+        for dc, y, z, mask, sem in transfers:
+            cast = codes if x else ap
+            out.append(RemoteDMATransfer(dst_ids=[_dst(topo, c, core) for c in dc], dma_engine_mask=mask, remote_sem=T.sem[sem],
+                                         srcs=[cast(z)], dsts=[cast(y) for c in dc]))
+            n += bin(mask).count("1")
+        g.remote_dma_fused(out, local_sem=T.sem[s])
+        note("g", [t[2] for t in transfers], [], (s, n), True)
+        ends.append((s, n))
+
+    others = [d for d in range(NR) if d != me]
+    oc_ = [T.cores[d] for d in others]
+    helper = _helper_of(topo, core)
+    engs = topo.engines(core, oc_[0])
+    m_all = topo.mask(core, oc_[0])
+    m_help = topo.mask(core, helper)
+    bcast = 2 * len(engs) * (NR - 1)
+
+    smn = [0]
+
+    def sm(n=1):
+        smn[0] += n
+        return ("SM", smn[0] - n, smn[0], 1)
+
+    dma("s", v("TB"), v("TB"), None, T.tb[:, :])
+    dma("a", v("UC"), v("UC"), None, T.u[:, 0:4])
+    dma("a", v("NZ"), v("NZ"), None, T.nz[:, :])
+    dma("s", v("WT"), v("WT"), None, T.w[:, :])
+
+    def iota(out, pattern, mult, small=True):
+        if small:
+            op("g", lambda: g.iota(ap(out), pattern, 0, mult, allow_small_or_imprecise_dtypes=True), [], [out])
+        else:
+            op("g", lambda: g.iota(ap(out), pattern, 0, mult), [], [out])
+
+    iota(v("CI", 0, 1), [[0, 1]], 1, False)
+    iota(v("KI"), [[1, 128]], 0)
+    iota(v("OH2"), [[0, 8], [1, 16], [16, 2]], 0)
+    iota(v("J32"), [[1, 32]], 0)
+    iota(v("IREF"), [[0, 8], [1, 16]], 0)
+    iota(v("QR"), [[0, 8], [1, 4], [0, 4]], 0)
+
+    ms(v("ZB"), 0.0)
+    act(v("MVC"), v("ZB", 0, 512))
+    act(v("HALF"), v("ZB", 0, 520), F.Identity, bias=0.5)
+    op("g", lambda: g.affine_select(ap(v("ZE")), ap(v("HALF")), [[1, 520]], A.is_equal, 0.0, -4, -4), [v("HALF")], [v("ZE")])
+    ci, cf, ck = (lambda i: v("CI", i, i + 1)), (lambda i: v("CF", i, i + 1)), (lambda i: v("CK", i, i + 1))
+    J8 = v("J32", 0, 8)
+    ts(ci(1), ci(0), 15, A.bitwise_and)
+    ts(ci(2), ci(0), 4, A.logical_shift_right)
+    ts(ci(3), ci(0), 31, A.bitwise_and)
+    ts(ci(4), ci(0), 3, A.bitwise_and)
+    ts(ci(5), ci(0), 2, A.logical_shift_right)
+    cp(v("CF", 0, 6), v("CI", 0, 6))
+    P, I16, S16, Q32, Q4, P4 = [cf(i) for i in range(6)]
+    ts(v("TIE"), v("KI"), P, A.is_lt, TINY, A.mult)
+    for h in range(2):
+        act(v("OHREF", h, 512, 2), v("OH2"))
+    ts(ck(1), S16, 16.0, A.mult)
+    for e, x in ((0, ck(1)), (1, I16), (10, ck(1)), (11, I16), (16, S16), (21, I16), (26, S16), (31, I16)):
+        act(v("MVC", e, e + 1), x)
+
+    ts(v("NUC"), v("UC"), -1.0, A.mult)
+    for b in range(4):
+        ts(v("UT", b, 512, 4), v("ZB", 0, 128), v("UC", b, b + 1), A.add)
+        act(v("NU", b, 512, 4), v("ZB", 0, 128), F.Identity, bias=v("NUC", b, b + 1))
+    act(v("INFO"), v("ZB", 0, 512))
+    quant(v("UQ"), v("UT"))
+
+    TQ = v("TQ")
+    quant(TQ, v("TB"))
+    send(True, [([helper], v("HT"), TQ, m_help, "arrh")])
+    quant(v("NUQ"), v("NU"))
+    PX, PS, PL, PF = v("PA", 0, 128), v("PB", 0, 128), v("PC", 0, 128), v("PD", 0, 144)
+    mm(PX, v("UQ"), TQ, True, False)
+    mm(PX, TQ, v("NUQ"), False, True)
+    mm(PS, TQ, v("UQ"))
+    quant(v("MVQ"), v("MVC"))
+    rk = sm()
+    tt(v("CMP"), PX, v("TIE"), A.is_lt)
+    red(rk, v("CMP"))
+    ts(v("OHT"), v("OHREF"), rk, A.is_equal)
+    quant(v("OHQ"), v("OHT"))
+    ts(v("INFO", 0, 1), v("PB", 0, 1), 0.0, A.is_gt)
+    mm(PL, v("OHQ"), v("MVQ"))
+    cp(v("OFF1"), v("PC", 0, 4))
+    cp(v("INFO", 4, 8), v("PC", 4, 8))
+    pick_s(v("L1S", 0, 16), TQ, v("OFF1", 0, 1))
+    quant(v("L1S", 16, 144), v("INFO"))
+    pick_c(v("L1S", 0, 16), TQ, v("OFF1", 0, 1))
+    own = v("LD1", SL * me, SL * me + SL)
+    send(True, [(oc_, own, v("L1S", 0, SL), m_all, "arr1")])
+    send(False, [(oc_, v("LD1s", own[1], own[2]), v("L1Ss", 0, SL), m_all, "arr1")])
+    send(False, [([helper], v("HTs"), v("TQs"), m_help, "arrh")])
+    dma("s", own, v("L1S", 0, SL), codes(own), codes(v("L1S", 0, SL)))
+    dma("s", v("LD1s", own[1], own[2]), v("L1Ss", 0, SL))
+    pown = v("PH1", 16 * me, 16 * me + 16)
+    town = v("TQ", 16 * me, 16 * me + 16)
+    dma("s", pown, town, codes(pown), codes(town))
+    dma("s", v("PH1s", pown[1], pown[2]), v("TQs", town[1], town[2]))
+    pick_s(v("NB", 144, 160), TQ, v("OFF1", 2, 3))
+    pick_c(v("NB", 144, 160), TQ, v("OFF1", 2, 3))
+
+    ms(v("Z32"), 0.0)
+    for b in range(4):
+        quant(v("EQ", 128 * b, 128 * b + 128), v("ZE", 4 - b, 516 - b))
+    E = [v("EQ", 128 * b, 128 * b + 128) for b in range(4)]
+    for t in (0, 1):
+        n = "NT%d" % t
+        act(v(n), v("ZB"))
+        for a in range(NR):
+            act(v(n, 72 * a, 72 * a + 64), v("NZ", 64 * t, 64 * t + 64))
+        quant(v("N%dQ" % t), v(n))
+        if t == 0:
+            act(v("ONE"), v("ZB", 0, 512))
+            ms(v("ONE", 0, 512, 4), 1.0)
+            quant(v("ONQ"), v("ONE"))
+    PVb = [v("PV", 512 * b, 512 * b + 144) for b in range(4)]
+    for b in range(4):
+        mm(PVb[b], E[b], v("N1Q"))
+    ms(v("NZ1", 64, 80), 0.0)
+    for b in range(4):
+        act(v("NZ1", b, 64, 4), v("PV", 512 * b, 512 * b + 16))
+    for b in range(4):
+        mm(PVb[b], E[b], v("N0Q"), True, False)
+    ts(v("TIE8"), J8, -0.125, A.mult, 0.875, A.add)
+    ts(v("W8"), J8, -8.0, A.add)
+    ts(ck(0), I16, float(SL * NR), A.add)
+    ms(v("KR"), -1.0)
+    ms(v("KR1"), -1.0)
+
+    landed("LD1", 0, own[1], ("arr1", bcast))
+    landed("LD1", own[2], 144, ("arr1", bcast))
+    mm(PF, v("ONQ"), v("LD1"))
+    for b in range(4):
+        mm(PVb[b], E[b], v("LD1"), False, True)
+    for b in range(4):
+        act(v("V0", b, 576, 4), PVb[b])
+    FIT = v("PD", 16, 144, SL)
+
+    def places(kr, kt, rep, pr):
+        pl, c8 = sm(), sm(8)
+        tr(v(kt), v(kr))
+        ts(c8, v(kr, 0, 8), v(kt, 0, 1), A.is_gt)
+        red(pl, c8)
+        ts(v(rep), v("Z32"), pl, A.add)
+        tr(v(pr), v(rep))
+        return pl
+
+    tt(v("KR", 0, 8), FIT, v("TIE8"), A.add)
+    pl0 = places("KR", "KT", "REP", "PR")
+    PR = v("PR", 0, 8)
+    plm = v("PR", me, me + 1)
+    e8, w8, tk18, gm = sm(8), sm(8), sm(), sm()
+    ts(e8, PR, plm, A.add, 7.0, A.is_equal)
+    ts(tk18, plm, 3.5, A.is_gt, float(SL), A.mult)
+    tt(w8, e8, v("W8"), A.mult)
+    red(gm, w8)
+    ts(v("OFFH", 0, 1), gm, tk18, A.mult, ck(0), A.add)
+    quant(v("NB", 0, 144), v("V0"))
+    hown = v("W2", 128 + 16 * me, 144 + 16 * me)
+    pick_c(hown, v("NB"), v("OFFH", 0, 1))
+    pick_s(hown, v("NB"), v("OFFH", 0, 1))
+    hos = v("W2s", hown[1], hown[2])
+    send(True, [(oc_, hown, hown, m_all, "arr2")])
+    send(False, [(oc_, hos, hos, m_all, "arr2")])
+
+    for b in range(4):
+        mm(PVb[b], E[b], v("N1Q"), True, False)
+        mm(PVb[b], E[b], v("LD1"), False, True)
+    for b in range(4):
+        act(v("V1", b, 576, 4), PVb[b])
+    F0, TK, t1, TGc, E0, q8, BSc, FBc, PAR, CAP, KB = sm(8), sm(8), sm(), sm(), sm(8), sm(8), sm(), sm(), sm(8), sm(8), sm(8)
+    cp(F0, FIT)
+    ts(TK, PR, 3.5, A.is_gt)
+    ts(t1, pl0, -1.0, A.mult, 7.0, A.add)
+    tt(TGc, pl0, t1, A.min)
+    ts(E0, PR, TGc, A.is_equal)
+    tt(q8, E0, F0, A.mult)
+    red(FBc, q8)
+    q8b = sm(8)
+    tt(q8b, E0, J8, A.mult)
+    red(BSc, q8b)
+    ts(v("REPF"), v("Z32"), FBc, A.add)
+    tr(v("FBR"), v("REPF"))
+    ts(v("REPB"), v("Z32"), BSc, A.add)
+    tr(v("BR0"), v("REPB"))
+    BR = v("BR0", 0, 8)
+    ts(CAP, TK, -1000.0, A.mult, 1112.0, A.add)
+    tt(CAP, v("FBR", 0, 8), CAP, A.min)
+    tt(KB, CAP, v("TIE8"), A.add)
+    ts(v("OFT"), J8, 0.0, A.add)
+    ts(v("TH8"), TK, -BIG, A.mult, BIG, A.add)
+    op("v", lambda: g.vector.tensor_copy(ap(v("THR")), ap(v("TH8")).indirect(ap(v("OFT")))), [v("TH8"), v("OFT")], [v("THR")])
+    ts(v("RM"), v("IREF"), 0.0, A.is_gt)
+    quant(v("W2", 384, 528), v("V1"))
+    ts(v("MS"), J8, S16, A.is_equal)
+    ts(PAR, PR, -1.0, A.mult, 7.0, A.add)
+    tt(PAR, PAR, PR, A.min)
+    TKp, BSp, PAp, HIp, LOp, Zp, D1 = sm(), sm(), sm(), sm(), sm(), sm(), sm()
+    for out, row in ((TKp, TK), (BSp, BR), (PAp, PAR)):
+        x8 = sm(8)
+        tt(x8, row, v("MS"), A.mult)
+        red(out, x8)
+    sl, s0, s1 = sm(8), sm(8), sm(8)
+    ts(sl, J8, BSp, A.is_equal, 2.0, A.mult)
+    ts(s0, sl, TKp, A.mult)
+    tt(s1, sl, s0, A.subtract)
+    for out, e in ((HIp, 68), (LOp, 69)):
+        x16 = sm(16)
+        tt(("SM", x16[1], x16[1] + 8, 1), s0, v("V0", e, 576, 72), A.mult)
+        tt(("SM", x16[1] + 8, x16[1] + 16, 1), s1, v("V0", e + 2, 576, 72), A.mult)
+        red(out, x16)
+    act(v("ZT"), v("ZB", 0, 512))
+    act(v("ZW"), v("ZB", 0, 512))
+    ts(v("DIAG"), v("KI"), P, A.is_equal)
+    for b, x in ((0, HIp), (1, LOp), (2, PAp)):
+        act(v("ZT", b, 512, 4), v("DIAG"), F.Identity, scale=x)
+    for b, x in ((0, 16.0), (1, 1.0), (2, 256.0)):
+        ms(v("ZW", b, 512, 4), x)
+    quant(v("ZWQ"), v("ZW"))
+    ts(Zp, HIp, 16.0, A.mult, LOp, A.add)
+    ts(Zp, PAp, 256.0, A.mult, Zp, A.add)
+    quant(v("ZQ"), v("ZT"))
+    mm(PL, v("ZWQ"), v("ZQ"))
+    ts(v("DD"), PL, Zp, A.subtract)
+    tt(v("SQ"), v("DD"), v("DD"), A.mult)
+    ts(v("TA"), v("DD"), 0.0, A.is_lt, TINY, A.mult)
+    ts(v("SQ"), v("SQ"), 16400.0, A.is_gt, -BIG, A.mult)
+    tt(v("TI1"), v("TA"), v("SQ"), A.add)
+
+    landed("W2", 128, hown[1], ("arr2", bcast))
+    landed("W2", hown[2], 256, ("arr2", bcast))
+    H = v("W2", 128, 256)
+    mm(PS, v("UQ"), H)
+    mm(PX, v("UQ"), H, True, False)
+    mm(PX, H, v("NUQ"), False, True)
+    for b in range(4):
+        mm(v("PV", 512 * b, 512 * b + 128), E[b], H)
+    for b in range(4):
+        act(v("D5", b, 512, 4), v("PV", 512 * b, 512 * b + 128))
+    tt(v("IND"), PS, v("THR"), A.is_gt)
+    op("v", lambda: g.vector.tensor_tensor_scan(ap(v("CS")), ap(v("RM")), ap(v("IND")), 0.0, A.mult, A.add), [v("RM"), v("IND")], [v("CS")])
+    tt(v("KR1", 0, 8), v("CS", 15, 128, 16), KB, A.add)
+    pl1 = places("KR1", "KT1", "RE1", "PR1")
+    P1 = v("PR1", 0, 8)
+    t2, TG1, E1, r8, fc = sm(), sm(), sm(8), sm(8), sm()
+    ts(t2, pl1, -1.0, A.mult, 7.0, A.add)
+    tt(TG1, pl1, t2, A.min)
+    ts(E1, P1, TG1, A.is_equal)
+    tt(r8, E1, BR, A.mult)
+    red(fc, r8)
+    ts(v("RE2"), v("Z32"), fc, A.add)
+    tr(v("FR"), v("RE2"))
+    ts(v("OFF3"), v("FR", 0, 8), 16.0, A.mult, I16, A.add)
+    landed("PH1", 0, pown[1], ("arrp", 2 * (NR - 1)))
+    landed("PH1", pown[2], 128, ("arrp", 2 * (NR - 1)))
+    pick_s(v("S3"), v("PH1"), v("OFF3"))
+    pick_c(v("S3"), v("PH1"), v("OFF3"))
+    bown = v("W2", 16 * me, 16 * me + 16)
+    send(True, [([c], bown, v("S3", 16 * d, 16 * d + 16), 1 << engs[i], "arr3") for i, (d, c) in enumerate(zip(others, oc_))])
+    send(False, [([c], v("W2s", bown[1], bown[2]), v("S3s", 16 * d, 16 * d + 16), 1 << engs[i], "arr3") for i, (d, c) in enumerate(zip(others, oc_))])
+    ts(v("OFFO", 0, 1), v("FR", me, me + 1), 16.0, A.mult, I16, A.add)
+    pick_c(bown, v("PH1"), v("OFFO", 0, 1))
+    pick_s(bown, v("PH1"), v("OFFO", 0, 1))
+
+    Mp = sm()
+    tt(v("CM1"), PX, v("TI1"), A.is_lt)
+    red(Mp, v("CM1"))
+    act(v("MT"), v("ZB", 0, 512))
+    act(v("ST4"), v("ZB", 0, 512))
+    act(v("NT"), v("ZB", 0, 512))
+    ts(v("M32"), v("J32"), P4, A.is_equal)
+    ts(v("MT", 0, 128, 4), v("M32"), Mp, A.mult, 16.0, A.min)
+    quant(v("MQ"), v("MT"))
+    ts(v("ST4", 0, 512, 4), v("QR"), Q4, A.is_equal, 4.0, A.mult)
+    quant(v("S4Q"), v("ST4"))
+    mm(PL, v("S4Q"), v("MQ"))
+    ts(v("OHL"), v("IREF"), LOp, A.is_equal)
+    for b, x in ((0, 16.0), (1, 1.0), (2, 128.0), (3, 1.0)):
+        act(v("STT", b, 512, 4), v("OHL"), F.Identity, scale=x)
+    ts(v("OFFG"), v("PC", 0, 32), Q4, A.add)
+    op("v", lambda: g.vector.tensor_tensor(ap(v("VT")), ap(v("NZ1", 0, 72)).indirect(ap(v("OFFG"))), ap(v("D5")), A.add),
+       [v("NZ1", 0, 72), v("OFFG"), v("D5")], [v("VT")])
+    quant(v("W2", 256, 384), v("VT"))
+    quant(v("STQ"), v("STT"))
+    p1m = v("PR1", me, me + 1)
+    T1, tg, em, Am, PTm, PAm = sm(), sm(), sm(8), sm(), sm(), sm()
+    ts(T1, p1m, 3.5, A.is_gt)
+    ts(tg, p1m, -1.0, A.mult, 7.0, A.add)
+    tt(tg, tg, p1m, A.min)
+    ts(em, P1, tg, A.is_equal)
+    for out, row in ((Am, J8), (PTm, TK), (PAm, PAR)):
+        x8 = sm(8)
+        tt(x8, em, row, A.mult)
+        red(out, x8)
+    c1, c2, nk, cc, M16, D2, D0, D3, sel, G, D2b = sm(), sm(), sm(), sm(), sm(), sm(), sm(), sm(), sm(), sm(8), sm()
+    tt(c1, T1, PTm, A.mult)
+    tt(c2, T1, c1, A.subtract)
+    tt(cc, c2, TKp, A.mult)
+    tt(nk, c2, PTm, A.add)
+    ts(nk, nk, -1.0, A.mult, 1.0, A.add)
+    tt(nk, nk, TKp, A.mult)
+    ts(sel, PAp, PAm, A.is_equal)
+    tt(D2, sel, nk, A.mult)
+    tt(sel, sel, D2, A.subtract)
+    ts(M16, Mp, 15.5, A.is_lt)
+    tt(D2b, c1, M16, A.mult)
+    ts(D2b, cc, 2.0, A.mult, D2b, A.add)
+    ts(D2b, D2b, 1.0, A.add)
+    tt(D0, Am, S16, A.subtract)
+    tt(D0, D0, cc, A.mult)
+    tt(D0, D0, S16, A.add)
+    tt(D0, D0, HIp, A.subtract)
+    tt(D1, I16, LOp, A.subtract)
+    tt(D3, Am, cc, A.mult)
+    ts(D3, D3, 2.0, A.mult)
+    ts(G, J8, HIp, A.is_equal, sel, A.mult)
+    for b, x in enumerate((D0, D1, D2b, D3)):
+        ts(v("NT", b, 32, 4), G, x, A.mult)
+    quant(v("NTQ"), v("NT"))
+    mm(v("PD", 0, 128), v("STQ"), v("NTQ"))
+    fl = sm(8)
+    ts(v("JC"), J8, 16.0, A.mult, I16, A.add)
+    tt(fl, v("PD", 0, 8), v("JC"), A.add)
+    cp(v("OFFF"), fl)
+    quant(v("WQ"), v("WT"))
+    for t, pr in ((0, PR), (1, P1)):
+        x8, xc = sm(8), sm()
+        ts(x8, pr, Q32, A.is_equal)
+        tt(x8, x8, J8, A.mult)
+        red(xc, x8)
+        ts(v("RO%d" % t), v("Z32"), xc, A.add)
+        tr(v("OD%d" % t), v("RO%d" % t))
+        o = v("OD%d" % t)[1]
+        dma("s", ("od", 0, 1, 1), v("OD%d" % t), T.od[t:t + 1, :], T.R32[0:1, o:o + 8])
+
+    landed("W2", 0, bown[1], ("arr3", 2 * (NR - 1)))
+    landed("W2", bown[2], 128, ("arr3", 2 * (NR - 1)))
+    pick_c(v("FT"), v("W2"), v("OFFF"))
+    pick_s(v("FT"), v("W2"), v("OFFF"))
+    dma("s", ("oc", 0, 1, 1), v("FT"), T.oc[:, :], codes(v("FT")))
+    mm(PS, v("WQ"), v("FT"))
+    for k in range(4):
+        dma("a", ("osc", 0, 1, 1), v("FTs"), T.osc[4 * k:4 * k + 4, :], T.FTs[32 * k:32 * k + 4, 0:128])
+    cp(v("Y"), PS)
+    dma("s", ("y", 0, 1, 1), v("Y"), T.y[:, :])
+
+    for q in ("v", "a", "t", "g"):
+        g.wait_ge(T.sem[SEM[q]], cnt[q])
+    for s, n in ends:
+        g.wait_ge(T.sem[s], n)

@@ -19,12 +19,12 @@ SCRATCH = {}
 for _n, _w, _t in (
         ("TB", 512, _b), ("UC", 4, _b), ("NUC", 4, _b), ("NZ", 128, _b), ("WT", 512, _b), ("ZB", 576, _b), ("UT", 512, _b), ("NU", 512, _b),
         ("CI", 8, "int32"), ("CF", 8, _f), ("CK", 16, _f), ("J32", 32, _f), ("KI", 128, _b), ("IREF", 128, _b), ("OH2", 256, _b),
-        ("OHREF", 512, _b), ("QR", 128, _b), ("HALF", 520, _b), ("ZE", 520, _b), ("TIE", 128, _f), ("DIAG", 128, _f), ("RM", 128, _f),
+        ("OHREF", 512, _b), ("QR", 128, _b), ("ZE", 520, _b), ("TIE", 128, _f), ("DIAG", 128, _f), ("RM", 128, _f),
         ("M32", 32, _f), ("MS", 8, _f), ("JC", 8, _f), ("TIE8", 8, _f), ("W8", 8, _f), ("Z32", 32, _f),
         ("MVC", 512, _b), ("ONE", 512, _b), ("ZW", 512, _b), ("ST4", 512, _b), ("NT0", 576, _b), ("NT1", 576, _b),
         ("INFO", 512, _b), ("OHT", 512, _b), ("CMP", 128, _f), ("SM", 384, _f), ("R32", 32 * len(ROWS), _f),
-        ("V0", 576, _b), ("V1", 576, _b), ("NZ1", 80, _f), ("TH8", 8, _f), ("THR", 128, _f), ("ZT", 512, _b),
-        ("DD", 128, _f), ("SQ", 128, _f), ("TI1", 128, _f), ("TA", 128, _f), ("IND", 128, _f), ("CS", 128, _f),
+        ("V0", 576, _b), ("V1", 576, _b), ("NZ1", 80, _f), ("TH8", 8, _f), ("PA8", 8, _f), ("THR", 128, _f), ("ZT", 512, _b),
+        ("TI1", 128, _f), ("TA", 128, _f), ("IND", 128, _f), ("CS", 128, _f),
         ("D5", 512, _f), ("MT", 512, _b), ("VT", 512, _b), ("OHL", 128, _b), ("STT", 512, _b), ("NT", 512, _b), ("Y", 128, _f), ("CM1", 128, _f),
         ("OFF1", 4, _u), ("OFFH", 2, _u), ("OFF3", 8, _u), ("OFFO", 2, _u), ("OFFG", 32, _u), ("OFFF", 8, _u), ("OFT", 8, _u)):
     SCRATCH[_n] = ("sbuf", [128, _w], _t)
@@ -35,7 +35,7 @@ for _n, _w in (("UQ", 128), ("NUQ", 128), ("TQ", 128), ("MVQ", 128), ("OHQ", 128
 for _n, _w in (("PV", 2048), ("PA", 512), ("PB", 512), ("PC", 512), ("PD", 512)):
     SCRATCH[_n] = ("psum", [128, _w], _f)
 
-SEMAPHORES = ["sv", "sa", "st", "sg", "arrh", "arr1", "arr2", "arr3", "arrp"]
+SEMAPHORES = ["sv", "sa", "st", "sg", "arrh", "arrg", "arr1", "arr2", "arr3", "arrp"]
 SEMAPHORES += ["d%d" % i for i in range(24)] + ["l%d" % i for i in range(12)]
 
 
@@ -50,10 +50,11 @@ def _dst(topo, d, s):
 
 def _hand_on(g, core, T, topo, owner):
     me = T.rank_of(owner)
-    g.wait_ge(T.sem.arrh, 2 * len(topo.engines(owner, core)))
-    for k, (src, dst) in enumerate((("HT", "PH1"), ("HTs", "PH1s"))):
+    near, far = topo.engines(owner, core), len(topo.engines(owner, T.cores[me - 1]))
+    for k, (src, dst, sem, n) in enumerate((("HT", "PH1", "arrh", len(near)), ("HTs", "PH1s", "arrg", len(near) - far))):
+        g.wait_ge(T.sem[sem], n)
         tr = []
-        for i, d in enumerate(x for x in range(NR) if x != me):
+        for i, d in enumerate((me + x) % NR for x in range(1, NR)):
             c = T.cores[d]
             s, t = T[src][:, 16 * d:16 * d + 16], T[dst][:, 16 * me:16 * me + 16]
             if k == 0:
@@ -167,6 +168,9 @@ def rank_program(g, core, T, topo):
         ws, xs = v(w[0] + "s", w[1], w[2]), v(x[0] + "s", x[1], x[2])
         op("t", lambda: g.tensor.matmul_mx(ap(out), ap(w), ap(ws), ap(x), ap(xs), start, stop), [w, ws, x, xs], [out])
 
+    def spread(out, win):
+        op("v", lambda: g.vector.tensor_copy(ap(out), ap(win).indirect(ap(v("OFT")))), [win, v("OFT")], [out])
+
     def pick_c(out, win, off):
         op("v", lambda: g.vector.tensor_copy(ap(out).bitcast(dt.uint32), ap(win).bitcast(dt.uint32).indirect(ap(off))), [win, off], [out])
 
@@ -204,12 +208,13 @@ def rank_program(g, core, T, topo):
         note("g", [t[2] for t in transfers], [], (s, n), True)
         ends.append((s, n))
 
-    others = [d for d in range(NR) if d != me]
+    others = [(me + i) % NR for i in range(1, NR)]
     oc_ = [T.cores[d] for d in others]
     helper = _helper_of(topo, core)
     engs = topo.engines(core, oc_[0])
     m_all = topo.mask(core, oc_[0])
     m_help = topo.mask(core, helper)
+    m_far = m_help & ~m_all
     bcast = 2 * len(engs) * (NR - 1)
 
     smn = [0]
@@ -234,12 +239,9 @@ def rank_program(g, core, T, topo):
     iota(v("OH2"), [[0, 8], [1, 16], [16, 2]], 0)
     iota(v("J32"), [[1, 32]], 0)
     iota(v("IREF"), [[0, 8], [1, 16]], 0)
-    iota(v("QR"), [[0, 8], [1, 4], [0, 4]], 0)
 
     ms(v("ZB"), 0.0)
     act(v("MVC"), v("ZB", 0, 512))
-    act(v("HALF"), v("ZB", 0, 520), F.Identity, bias=0.5)
-    op("g", lambda: g.affine_select(ap(v("ZE")), ap(v("HALF")), [[1, 520]], A.is_equal, 0.0, -4, -4), [v("HALF")], [v("ZE")])
     ci, cf, ck = (lambda i: v("CI", i, i + 1)), (lambda i: v("CF", i, i + 1)), (lambda i: v("CK", i, i + 1))
     J8 = v("J32", 0, 8)
     ts(ci(1), ci(0), 15, A.bitwise_and)
@@ -261,6 +263,7 @@ def rank_program(g, core, T, topo):
         ts(v("UT", b, 512, 4), v("ZB", 0, 128), v("UC", b, b + 1), A.add)
         act(v("NU", b, 512, 4), v("ZB", 0, 128), F.Identity, bias=v("NUC", b, b + 1))
     act(v("INFO"), v("ZB", 0, 512))
+    act(v("ZE"), v("ZB", 0, 520))
     quant(v("UQ"), v("UT"))
 
     TQ = v("TQ")
@@ -287,7 +290,7 @@ def rank_program(g, core, T, topo):
     own = v("LD1", SL * me, SL * me + SL)
     send(True, [(oc_, own, v("L1S", 0, SL), m_all, "arr1")])
     send(False, [(oc_, v("LD1s", own[1], own[2]), v("L1Ss", 0, SL), m_all, "arr1")])
-    send(False, [([helper], v("HTs"), v("TQs"), m_help, "arrh")])
+    send(False, [([helper], v("HTs"), v("TQs"), m_far, "arrg")])
     dma("s", own, v("L1S", 0, SL), codes(own), codes(v("L1S", 0, SL)))
     dma("s", v("LD1s", own[1], own[2]), v("L1Ss", 0, SL))
     pown = v("PH1", 16 * me, 16 * me + 16)
@@ -297,7 +300,9 @@ def rank_program(g, core, T, topo):
     pick_s(v("NB", 144, 160), TQ, v("OFF1", 2, 3))
     pick_c(v("NB", 144, 160), TQ, v("OFF1", 2, 3))
 
+    iota(v("QR"), [[0, 8], [1, 4], [0, 4]], 0)
     ms(v("Z32"), 0.0)
+    ts(v("ZE", 4, 516, 4), v("KI"), P, A.is_equal, 0.5, A.mult)
     for b in range(4):
         quant(v("EQ", 128 * b, 128 * b + 128), v("ZE", 4 - b, 516 - b))
     E = [v("EQ", 128 * b, 128 * b + 128) for b in range(4)]
@@ -324,6 +329,14 @@ def rank_program(g, core, T, topo):
     ts(ck(0), I16, float(SL * NR), A.add)
     ms(v("KR"), -1.0)
     ms(v("KR1"), -1.0)
+    ts(v("OFT"), J8, 0.0, A.add)
+    ts(v("RM"), v("IREF"), 0.0, A.is_gt)
+    ts(v("MS"), J8, S16, A.is_equal)
+    ts(v("DIAG"), v("KI"), P, A.is_equal)
+    ms(v("ZW"), 0.0)
+    for b, x in ((0, 16.0), (1, 1.0)):
+        ms(v("ZW", b, 512, 4), x)
+    quant(v("ZWQ"), v("ZW"))
 
     landed("LD1", 0, own[1], ("arr1", bcast))
     landed("LD1", own[2], 144, ("arr1", bcast))
@@ -367,33 +380,30 @@ def rank_program(g, core, T, topo):
     for b in range(4):
         act(v("V1", b, 576, 4), PVb[b])
     F0, TK, t1, TGc, E0, q8, BSc, FBc, PAR, CAP, KB = sm(8), sm(8), sm(), sm(), sm(8), sm(8), sm(), sm(), sm(8), sm(8), sm(8)
+    q8b = sm(8)
     cp(F0, FIT)
     ts(TK, PR, 3.5, A.is_gt)
     ts(t1, pl0, -1.0, A.mult, 7.0, A.add)
     tt(TGc, pl0, t1, A.min)
     ts(E0, PR, TGc, A.is_equal)
     tt(q8, E0, F0, A.mult)
-    red(FBc, q8)
-    q8b = sm(8)
     tt(q8b, E0, J8, A.mult)
+    red(FBc, q8)
     red(BSc, q8b)
     ts(v("REPF"), v("Z32"), FBc, A.add)
-    tr(v("FBR"), v("REPF"))
     ts(v("REPB"), v("Z32"), BSc, A.add)
+    tr(v("FBR"), v("REPF"))
     tr(v("BR0"), v("REPB"))
     BR = v("BR0", 0, 8)
     ts(CAP, TK, -1000.0, A.mult, 1112.0, A.add)
     tt(CAP, v("FBR", 0, 8), CAP, A.min)
     tt(KB, CAP, v("TIE8"), A.add)
-    ts(v("OFT"), J8, 0.0, A.add)
     ts(v("TH8"), TK, -BIG, A.mult, BIG, A.add)
-    op("v", lambda: g.vector.tensor_copy(ap(v("THR")), ap(v("TH8")).indirect(ap(v("OFT")))), [v("TH8"), v("OFT")], [v("THR")])
-    ts(v("RM"), v("IREF"), 0.0, A.is_gt)
+    spread(v("THR"), v("TH8"))
     quant(v("W2", 384, 528), v("V1"))
-    ts(v("MS"), J8, S16, A.is_equal)
     ts(PAR, PR, -1.0, A.mult, 7.0, A.add)
     tt(PAR, PAR, PR, A.min)
-    TKp, BSp, PAp, HIp, LOp, Zp, D1 = sm(), sm(), sm(), sm(), sm(), sm(), sm()
+    TKp, BSp, PAp, HIp, LOp, Zp = sm(), sm(), sm(), sm(), sm(), sm()
     for out, row in ((TKp, TK), (BSp, BR), (PAp, PAR)):
         x8 = sm(8)
         tt(x8, row, v("MS"), A.mult)
@@ -408,22 +418,32 @@ def rank_program(g, core, T, topo):
         tt(("SM", x16[1] + 8, x16[1] + 16, 1), s1, v("V0", e + 2, 576, 72), A.mult)
         red(out, x16)
     act(v("ZT"), v("ZB", 0, 512))
-    act(v("ZW"), v("ZB", 0, 512))
-    ts(v("DIAG"), v("KI"), P, A.is_equal)
-    for b, x in ((0, HIp), (1, LOp), (2, PAp)):
+    act(v("MT"), v("ZB", 0, 512))
+    for b, x in ((0, HIp), (1, LOp)):
         act(v("ZT", b, 512, 4), v("DIAG"), F.Identity, scale=x)
-    for b, x in ((0, 16.0), (1, 1.0), (2, 256.0)):
-        ms(v("ZW", b, 512, 4), x)
-    quant(v("ZWQ"), v("ZW"))
     ts(Zp, HIp, 16.0, A.mult, LOp, A.add)
-    ts(Zp, PAp, 256.0, A.mult, Zp, A.add)
+    ts(v("OHL"), v("IREF"), LOp, A.is_equal)
+    ts(v("PA8"), PAR, 0.0, A.add)
+    spread(v("TA"), v("PA8"))
     quant(v("ZQ"), v("ZT"))
     mm(PL, v("ZWQ"), v("ZQ"))
-    ts(v("DD"), PL, Zp, A.subtract)
-    tt(v("SQ"), v("DD"), v("DD"), A.mult)
-    ts(v("TA"), v("DD"), 0.0, A.is_lt, TINY, A.mult)
-    ts(v("SQ"), v("SQ"), 16400.0, A.is_gt, -BIG, A.mult)
-    tt(v("TI1"), v("TA"), v("SQ"), A.add)
+    for b, x in ((0, 16.0), (1, 1.0), (2, 128.0), (3, 1.0)):
+        act(v("STT", b, 512, 4), v("OHL"), F.Identity, scale=x)
+    act(v("NT"), v("ZB", 0, 512))
+    ts(v("TA"), v("TA"), PAp, A.not_equal, -BIG, A.mult)
+    ts(v("TI1"), PL, Zp, A.is_lt, TINY, A.mult)
+    tt(v("TI1"), v("TI1"), v("TA"), A.add)
+    D0, D1, X0, X3, TK2 = sm(), sm(), sm(), sm(), sm()
+    ts(D0, S16, HIp, A.subtract, 8.0, A.add)
+    tt(D1, I16, LOp, A.subtract)
+    ts(X0, BSp, S16, A.subtract, TKp, A.mult)
+    ts(X3, BSp, 2.0, A.mult, TKp, A.mult)
+    ts(TK2, TKp, 2.0, A.mult)
+    ts(v("M32"), v("J32"), P4, A.is_equal)
+    ts(v("JC"), J8, 16.0, A.mult, I16, A.add)
+    ms(v("ST4"), 0.0)
+    ts(v("ST4", 0, 512, 4), v("QR"), Q4, A.is_equal, 4.0, A.mult)
+    quant(v("S4Q"), v("ST4"))
 
     landed("W2", 128, hown[1], ("arr2", bcast))
     landed("W2", hown[2], 256, ("arr2", bcast))
@@ -463,61 +483,40 @@ def rank_program(g, core, T, topo):
     Mp = sm()
     tt(v("CM1"), PX, v("TI1"), A.is_lt)
     red(Mp, v("CM1"))
-    act(v("MT"), v("ZB", 0, 512))
-    act(v("ST4"), v("ZB", 0, 512))
-    act(v("NT"), v("ZB", 0, 512))
-    ts(v("M32"), v("J32"), P4, A.is_equal)
     ts(v("MT", 0, 128, 4), v("M32"), Mp, A.mult, 16.0, A.min)
     quant(v("MQ"), v("MT"))
-    ts(v("ST4", 0, 512, 4), v("QR"), Q4, A.is_equal, 4.0, A.mult)
-    quant(v("S4Q"), v("ST4"))
     mm(PL, v("S4Q"), v("MQ"))
-    ts(v("OHL"), v("IREF"), LOp, A.is_equal)
-    for b, x in ((0, 16.0), (1, 1.0), (2, 128.0), (3, 1.0)):
-        act(v("STT", b, 512, 4), v("OHL"), F.Identity, scale=x)
+    quant(v("STQ"), v("STT"))
     ts(v("OFFG"), v("PC", 0, 32), Q4, A.add)
     op("v", lambda: g.vector.tensor_tensor(ap(v("VT")), ap(v("NZ1", 0, 72)).indirect(ap(v("OFFG"))), ap(v("D5")), A.add),
        [v("NZ1", 0, 72), v("OFFG"), v("D5")], [v("VT")])
     quant(v("W2", 256, 384), v("VT"))
-    quant(v("STQ"), v("STT"))
     p1m = v("PR1", me, me + 1)
-    T1, tg, em, Am, PTm, PAm = sm(), sm(), sm(8), sm(), sm(), sm()
-    ts(T1, p1m, 3.5, A.is_gt)
+    T1, tg, em, PTm, PAm, xa, xb = sm(), sm(), sm(8), sm(), sm(), sm(8), sm(8)
     ts(tg, p1m, -1.0, A.mult, 7.0, A.add)
+    ts(T1, p1m, 3.5, A.is_gt)
     tt(tg, tg, p1m, A.min)
     ts(em, P1, tg, A.is_equal)
-    for out, row in ((Am, J8), (PTm, TK), (PAm, PAR)):
-        x8 = sm(8)
-        tt(x8, em, row, A.mult)
-        red(out, x8)
-    c1, c2, nk, cc, M16, D2, D0, D3, sel, G, D2b = sm(), sm(), sm(), sm(), sm(), sm(), sm(), sm(), sm(), sm(8), sm()
+    tt(xa, em, TK, A.mult)
+    tt(xb, em, PAR, A.mult)
+    red(PTm, xa)
+    red(PAm, xb)
+    c1, c2, nw, nk, sel, G, r1, D2, Y0, D3 = sm(), sm(), sm(), sm(), sm(), sm(8), sm(), sm(), sm(), sm()
     tt(c1, T1, PTm, A.mult)
+    ts(r1, Mp, 15.5, A.is_lt, c1, A.mult)
     tt(c2, T1, c1, A.subtract)
-    tt(cc, c2, TKp, A.mult)
-    tt(nk, c2, PTm, A.add)
-    ts(nk, nk, -1.0, A.mult, 1.0, A.add)
-    tt(nk, nk, TKp, A.mult)
-    ts(sel, PAp, PAm, A.is_equal)
-    tt(D2, sel, nk, A.mult)
-    tt(sel, sel, D2, A.subtract)
-    ts(M16, Mp, 15.5, A.is_lt)
-    tt(D2b, c1, M16, A.mult)
-    ts(D2b, cc, 2.0, A.mult, D2b, A.add)
-    ts(D2b, D2b, 1.0, A.add)
-    tt(D0, Am, S16, A.subtract)
-    tt(D0, D0, cc, A.mult)
-    tt(D0, D0, S16, A.add)
-    tt(D0, D0, HIp, A.subtract)
-    tt(D1, I16, LOp, A.subtract)
-    tt(D3, Am, cc, A.mult)
-    ts(D3, D3, 2.0, A.mult)
+    ts(nw, c2, PTm, A.add, -1.0, A.add)
+    ts(Y0, X0, c2, A.mult, D0, A.add)
+    ts(D3, X3, c2, A.mult)
+    ts(nk, TKp, nw, A.mult, 1.0, A.add)
+    ts(D2, TK2, c2, A.mult, r1, A.add)
+    ts(sel, PAp, PAm, A.is_equal, nk, A.mult)
     ts(G, J8, HIp, A.is_equal, sel, A.mult)
-    for b, x in enumerate((D0, D1, D2b, D3)):
+    for b, x in enumerate((Y0, D1, D2, D3)):
         ts(v("NT", b, 32, 4), G, x, A.mult)
     quant(v("NTQ"), v("NT"))
     mm(v("PD", 0, 128), v("STQ"), v("NTQ"))
     fl = sm(8)
-    ts(v("JC"), J8, 16.0, A.mult, I16, A.add)
     tt(fl, v("PD", 0, 8), v("JC"), A.add)
     cp(v("OFFF"), fl)
     quant(v("WQ"), v("WT"))

@@ -4,7 +4,8 @@ from concourse.mybir import dt, AluOpType, AxisListType, ActivationFunctionType
 A = AluOpType
 F = ActivationFunctionType
 NR, SL = 8, 18
-ROWS = ["KR", "KT", "REP", "PR", "REPB", "BR0", "REPF", "FBR", "KR1", "KT1", "RE1", "PR1", "RE2", "FR", "RO0", "OD0", "RO1", "OD1"]
+ROWS = {"KR": 32, "KT": 32, "KR1": 32, "KT1": 32, "FS": 16, "FBR": 16, "BR": 16, "B16": 16, "BS": 16, "A1": 16, "F16": 16, "J18": 16}
+RN = list(ROWS)
 TINY, BIG = 2.0 ** -100, 1e29
 
 _f, _b, _u = "float32", "bfloat16", "uint16"
@@ -20,13 +21,14 @@ for _n, _w, _t in (
         ("TB", 512, _b), ("UC", 4, _b), ("NUC", 4, _b), ("NZ", 128, _b), ("WT", 512, _b), ("ZB", 576, _b), ("UT", 512, _b), ("NU", 512, _b),
         ("CI", 8, "int32"), ("CF", 8, _f), ("CK", 16, _f), ("J32", 32, _f), ("KI", 128, _b), ("IREF", 128, _b), ("OH2", 256, _b),
         ("OHREF", 512, _b), ("QR", 128, _b), ("ZE", 520, _b), ("TIE", 128, _f), ("DIAG", 128, _f), ("RM", 128, _f),
-        ("M32", 32, _f), ("MS", 8, _f), ("JC", 8, _f), ("TIE8", 8, _f), ("W8", 8, _f), ("Z32", 32, _f),
+        ("M32", 32, _f), ("MS", 8, _f), ("JC", 8, _f), ("TIE8", 8, _f), ("WN", 32, _f), ("O0", 16, _f), ("O1", 16, _f),
         ("MVC", 512, _b), ("ONE", 512, _b), ("ZW", 512, _b), ("ST4", 512, _b), ("NT0", 576, _b), ("NT1", 576, _b),
         ("INFO", 512, _b), ("OHT", 512, _b), ("CMP", 128, _f), ("SM", 384, _f), ("R32", 32 * len(ROWS), _f),
-        ("V0", 576, _b), ("V1", 576, _b), ("NZ1", 80, _f), ("TH8", 8, _f), ("PA8", 8, _f), ("THR", 128, _f), ("ZT", 512, _b),
+        ("V0", 576, _b), ("V1", 576, _b), ("NZ1", 80, _f), ("TH8", 8, _f), ("THR", 128, _f), ("ZT", 512, _b),
         ("TI1", 128, _f), ("TA", 128, _f), ("IND", 128, _f), ("CS", 128, _f),
         ("D5", 512, _f), ("MT", 512, _b), ("VT", 512, _b), ("OHL", 128, _b), ("STT", 512, _b), ("NT", 512, _b), ("Y", 128, _f), ("CM1", 128, _f),
-        ("OFF1", 4, _u), ("OFFH", 2, _u), ("OFF3", 8, _u), ("OFFO", 2, _u), ("OFFG", 32, _u), ("OFFF", 8, _u), ("OFT", 8, _u)):
+        ("OFF1", 4, _u), ("OFFH", 18, _u), ("OFF3", 16, _u), ("OP0", 2, _u), ("OP1", 2, _u), ("OX0", 2, _u), ("TG0", 2, _u), ("TG1", 2, _u),
+        ("OFFO", 2, _u), ("OFFG", 32, _u), ("OFFF", 8, _u), ("OFT", 8, _u)):
     SCRATCH[_n] = ("sbuf", [128, _w], _t)
 for _n, _w in (("UQ", 128), ("NUQ", 128), ("TQ", 128), ("MVQ", 128), ("OHQ", 128), ("ONQ", 128), ("EQ", 512), ("N0Q", 144), ("N1Q", 144),
                ("WQ", 128), ("ZWQ", 128), ("S4Q", 128), ("L1S", 144), ("LD1", 144), ("NB", 160), ("W2", 528), ("PH1", 128), ("S3", 128),
@@ -118,8 +120,8 @@ def rank_program(g, core, T, topo):
 
     def v(n, lo=0, hi=None, st=1):
         if n in ROWS:
-            o = 32 * ROWS.index(n)
-            return ("R32", o + lo, o + (32 if hi is None else hi), st)
+            o = 32 * RN.index(n)
+            return ("R32", o + lo, o + (ROWS[n] if hi is None else hi), st)
         return (n, lo, SCRATCH[n][1][1] if hi is None else hi, st)
 
     def ap(x):
@@ -168,8 +170,14 @@ def rank_program(g, core, T, topo):
         ws, xs = v(w[0] + "s", w[1], w[2]), v(x[0] + "s", x[1], x[2])
         op("t", lambda: g.tensor.matmul_mx(ap(out), ap(w), ap(ws), ap(x), ap(xs), start, stop), [w, ws, x, xs], [out])
 
-    def spread(out, win):
-        op("v", lambda: g.vector.tensor_copy(ap(out), ap(win).indirect(ap(v("OFT")))), [win, v("OFT")], [out])
+    def scatter(out, in_, off):
+        op("v", lambda: g.vector.tensor_copy(ap(out).indirect(ap(off)), ap(in_)), [in_, off], [out])
+
+    def gather(out, win, off):
+        op("v", lambda: g.vector.tensor_copy(ap(out), ap(win).indirect(ap(off))), [win, off], [out])
+
+    def gather_add(out, win, off, col):
+        op("v", lambda: g.vector.tensor_scalar(ap(out), ap(win).indirect(ap(off)), ap(col), None, A.add), [win, off, col], [out])
 
     def pick_c(out, win, off):
         op("v", lambda: g.vector.tensor_copy(ap(out).bitcast(dt.uint32), ap(win).bitcast(dt.uint32).indirect(ap(off))), [win, off], [out])
@@ -228,11 +236,11 @@ def rank_program(g, core, T, topo):
     dma("a", v("NZ"), v("NZ"), None, T.nz[:, :])
     dma("s", v("WT"), v("WT"), None, T.w[:, :])
 
-    def iota(out, pattern, mult, small=True):
+    def iota(out, pattern, mult, small=True, base=0):
         if small:
-            op("g", lambda: g.iota(ap(out), pattern, 0, mult, allow_small_or_imprecise_dtypes=True), [], [out])
+            op("g", lambda: g.iota(ap(out), pattern, base, mult, allow_small_or_imprecise_dtypes=True), [], [out])
         else:
-            op("g", lambda: g.iota(ap(out), pattern, 0, mult), [], [out])
+            op("g", lambda: g.iota(ap(out), pattern, base, mult), [], [out])
 
     iota(v("CI", 0, 1), [[0, 1]], 1, False)
     iota(v("KI"), [[1, 128]], 0)
@@ -243,14 +251,14 @@ def rank_program(g, core, T, topo):
     ms(v("ZB"), 0.0)
     act(v("MVC"), v("ZB", 0, 512))
     ci, cf, ck = (lambda i: v("CI", i, i + 1)), (lambda i: v("CF", i, i + 1)), (lambda i: v("CK", i, i + 1))
-    J8 = v("J32", 0, 8)
+    J8, J16 = v("J32", 0, 8), v("J32", 0, 16)
     ts(ci(1), ci(0), 15, A.bitwise_and)
     ts(ci(2), ci(0), 4, A.logical_shift_right)
-    ts(ci(3), ci(0), 31, A.bitwise_and)
     ts(ci(4), ci(0), 3, A.bitwise_and)
     ts(ci(5), ci(0), 2, A.logical_shift_right)
+    ts(ci(3), ci(0), 31, A.bitwise_and)
     cp(v("CF", 0, 6), v("CI", 0, 6))
-    P, I16, S16, Q32, Q4, P4 = [cf(i) for i in range(6)]
+    P, I16, S16, Q4, P4 = cf(0), cf(1), cf(2), cf(4), cf(5)
     ts(v("TIE"), v("KI"), P, A.is_lt, TINY, A.mult)
     for h in range(2):
         act(v("OHREF", h, 512, 2), v("OH2"))
@@ -264,11 +272,11 @@ def rank_program(g, core, T, topo):
         act(v("NU", b, 512, 4), v("ZB", 0, 128), F.Identity, bias=v("NUC", b, b + 1))
     act(v("INFO"), v("ZB", 0, 512))
     act(v("ZE"), v("ZB", 0, 520))
-    quant(v("UQ"), v("UT"))
 
     TQ = v("TQ")
     quant(TQ, v("TB"))
     send(True, [([helper], v("HT"), TQ, m_help, "arrh")])
+    quant(v("UQ"), v("UT"))
     quant(v("NUQ"), v("NU"))
     PX, PS, PL, PF = v("PA", 0, 128), v("PB", 0, 128), v("PC", 0, 128), v("PD", 0, 144)
     mm(PX, v("UQ"), TQ, True, False)
@@ -285,8 +293,8 @@ def rank_program(g, core, T, topo):
     cp(v("OFF1"), v("PC", 0, 4))
     cp(v("INFO", 4, 8), v("PC", 4, 8))
     pick_s(v("L1S", 0, 16), TQ, v("OFF1", 0, 1))
-    quant(v("L1S", 16, 144), v("INFO"))
     pick_c(v("L1S", 0, 16), TQ, v("OFF1", 0, 1))
+    quant(v("L1S", 16, 144), v("INFO"))
     own = v("LD1", SL * me, SL * me + SL)
     send(True, [(oc_, own, v("L1S", 0, SL), m_all, "arr1")])
     send(False, [(oc_, v("LD1s", own[1], own[2]), v("L1Ss", 0, SL), m_all, "arr1")])
@@ -300,9 +308,11 @@ def rank_program(g, core, T, topo):
     pick_s(v("NB", 144, 160), TQ, v("OFF1", 2, 3))
     pick_c(v("NB", 144, 160), TQ, v("OFF1", 2, 3))
 
+    for n in ("KR", "KR1"):
+        iota(v(n), [[0, 2], [-1, 16]], 0, True, 7)
     iota(v("QR"), [[0, 8], [1, 4], [0, 4]], 0)
-    ms(v("Z32"), 0.0)
     ts(v("ZE", 4, 516, 4), v("KI"), P, A.is_equal, 0.5, A.mult)
+    ts(v("TIE8"), J8, -0.125, A.mult, 0.875, A.add)
     for b in range(4):
         quant(v("EQ", 128 * b, 128 * b + 128), v("ZE", 4 - b, 516 - b))
     E = [v("EQ", 128 * b, 128 * b + 128) for b in range(4)]
@@ -315,6 +325,8 @@ def rank_program(g, core, T, topo):
         if t == 0:
             act(v("ONE"), v("ZB", 0, 512))
             ms(v("ONE", 0, 512, 4), 1.0)
+            ts(v("J18"), J16, float(SL), A.mult)
+            ms(v("WN", 16, 32), float(SL * NR))
             quant(v("ONQ"), v("ONE"))
     PVb = [v("PV", 512 * b, 512 * b + 144) for b in range(4)]
     for b in range(4):
@@ -324,16 +336,12 @@ def rank_program(g, core, T, topo):
         act(v("NZ1", b, 64, 4), v("PV", 512 * b, 512 * b + 16))
     for b in range(4):
         mm(PVb[b], E[b], v("N0Q"), True, False)
-    ts(v("TIE8"), J8, -0.125, A.mult, 0.875, A.add)
-    ts(v("W8"), J8, -8.0, A.add)
-    ts(ck(0), I16, float(SL * NR), A.add)
-    ms(v("KR"), -1.0)
-    ms(v("KR1"), -1.0)
+    ms(v("F16"), 0.0)
     ts(v("OFT"), J8, 0.0, A.add)
     ts(v("RM"), v("IREF"), 0.0, A.is_gt)
     ts(v("MS"), J8, S16, A.is_equal)
-    ts(v("DIAG"), v("KI"), P, A.is_equal)
     ms(v("ZW"), 0.0)
+    ts(v("DIAG"), v("KI"), P, A.is_equal)
     for b, x in ((0, 16.0), (1, 1.0)):
         ms(v("ZW", b, 512, 4), x)
     quant(v("ZWQ"), v("ZW"))
@@ -347,29 +355,28 @@ def rank_program(g, core, T, topo):
         act(v("V0", b, 576, 4), PVb[b])
     FIT = v("PD", 16, 144, SL)
 
-    def places(kr, kt, rep, pr):
-        pl, c8 = sm(), sm(8)
+    def places(kr, kt, off):
+        pl, c16 = sm(), sm(16)
         tr(v(kt), v(kr))
-        ts(c8, v(kr, 0, 8), v(kt, 0, 1), A.is_gt)
-        red(pl, c8)
-        ts(v(rep), v("Z32"), pl, A.add)
-        tr(v(pr), v(rep))
+        ts(c16, v(kr, 0, 16), v(kt, 0, 1), A.is_gt)
+        red(pl, c16)
+        ts(v(off, 0, 1), pl, 0.0, A.add)
         return pl
 
-    tt(v("KR", 0, 8), FIT, v("TIE8"), A.add)
-    pl0 = places("KR", "KT", "REP", "PR")
-    PR = v("PR", 0, 8)
-    plm = v("PR", me, me + 1)
-    e8, w8, tk18, gm = sm(8), sm(8), sm(), sm()
-    ts(e8, PR, plm, A.add, 7.0, A.is_equal)
-    ts(tk18, plm, 3.5, A.is_gt, float(SL), A.mult)
-    tt(w8, e8, v("W8"), A.mult)
-    red(gm, w8)
-    ts(v("OFFH", 0, 1), gm, tk18, A.mult, ck(0), A.add)
+    for o in (0, 16):
+        tt(v("KR", o, o + 8), FIT, v("TIE8"), A.add)
+    pl0 = places("KR", "KT", "OP0")
+    gv = sm()
+    ts(gv, pl0, 3.5, A.is_lt, 16.0, A.mult)
+    scatter(v("WN", 0, 16), v("J18"), v("OP0", 0, 1))
+    ts(v("OX0", 0, 1), gv, pl0, A.subtract, 7.0, A.add)
+    sh = me % 2
+    gather_add(v("OFFH", sh, sh + 16), v("WN"), v("OX0", 0, 1), I16)
+    oh = v("OFFH", me + sh, me + sh + 1)
     quant(v("NB", 0, 144), v("V0"))
     hown = v("W2", 128 + 16 * me, 144 + 16 * me)
-    pick_c(hown, v("NB"), v("OFFH", 0, 1))
-    pick_s(hown, v("NB"), v("OFFH", 0, 1))
+    pick_c(hown, v("NB"), oh)
+    pick_s(hown, v("NB"), oh)
     hos = v("W2s", hown[1], hown[2])
     send(True, [(oc_, hown, hown, m_all, "arr2")])
     send(False, [(oc_, hos, hos, m_all, "arr2")])
@@ -379,70 +386,65 @@ def rank_program(g, core, T, topo):
         mm(PVb[b], E[b], v("LD1"), False, True)
     for b in range(4):
         act(v("V1", b, 576, 4), PVb[b])
-    F0, TK, t1, TGc, E0, q8, BSc, FBc, PAR, CAP, KB = sm(8), sm(8), sm(), sm(), sm(8), sm(8), sm(), sm(), sm(8), sm(8), sm(8)
-    q8b = sm(8)
-    cp(F0, FIT)
-    ts(TK, PR, 3.5, A.is_gt)
+    TK, t1, CAP, KB = sm(8), sm(), sm(8), sm(8)
     ts(t1, pl0, -1.0, A.mult, 7.0, A.add)
-    tt(TGc, pl0, t1, A.min)
-    ts(E0, PR, TGc, A.is_equal)
-    tt(q8, E0, F0, A.mult)
-    tt(q8b, E0, J8, A.mult)
-    red(FBc, q8)
-    red(BSc, q8b)
-    ts(v("REPF"), v("Z32"), FBc, A.add)
-    ts(v("REPB"), v("Z32"), BSc, A.add)
-    tr(v("FBR"), v("REPF"))
-    tr(v("BR0"), v("REPB"))
-    BR = v("BR0", 0, 8)
-    ts(CAP, TK, -1000.0, A.mult, 1112.0, A.add)
-    tt(CAP, v("FBR", 0, 8), CAP, A.min)
-    tt(KB, CAP, v("TIE8"), A.add)
+    cp(v("F16", 0, 8), FIT)
+    scatter(v("O0"), J16, v("OP0", 0, 1))
+    ts(v("TG0", 0, 1), t1, pl0, A.min)
+    scatter(v("FS"), v("F16"), v("OP0", 0, 1))
+    gather(v("BR"), v("O0"), v("TG0", 0, 1))
+    gather(v("FBR"), v("FS"), v("TG0", 0, 1))
+    BR = v("BR", 0, 8)
+    dma("s", ("od", 0, 1, 1), v("O0"), T.od[0:1, :], T.O0[0:1, 0:8])
+    TKp, BSp, HIp, LOp, Zp, xa, xb = sm(), sm(), sm(), sm(), sm(), sm(8), sm(8)
+    tt(TK, BR, J8, A.not_equal)
+    tt(xb, BR, v("MS"), A.mult)
+    ts(v("B16"), v("BR"), 16.0, A.mult)
     ts(v("TH8"), TK, -BIG, A.mult, BIG, A.add)
-    spread(v("THR"), v("TH8"))
-    quant(v("W2", 384, 528), v("V1"))
-    ts(PAR, PR, -1.0, A.mult, 7.0, A.add)
-    tt(PAR, PAR, PR, A.min)
-    TKp, BSp, PAp, HIp, LOp, Zp = sm(), sm(), sm(), sm(), sm(), sm()
-    for out, row in ((TKp, TK), (BSp, BR), (PAp, PAR)):
-        x8 = sm(8)
-        tt(x8, row, v("MS"), A.mult)
-        red(out, x8)
+    ts(CAP, TK, -1000.0, A.mult, 1112.0, A.add)
+    tt(xa, TK, v("MS"), A.mult)
+    red(BSp, xb)
+    gather(v("THR"), v("TH8"), v("OFT"))
+    tt(CAP, v("FBR", 0, 8), CAP, A.min)
+    red(TKp, xa)
     sl, s0, s1 = sm(8), sm(8), sm(8)
     ts(sl, J8, BSp, A.is_equal, 2.0, A.mult)
+    tt(KB, CAP, v("TIE8"), A.add)
+    ts(v("M32"), v("J32"), P4, A.is_equal)
     ts(s0, sl, TKp, A.mult)
+    gather(v("TA"), BR, v("OFT"))
     tt(s1, sl, s0, A.subtract)
-    for out, e in ((HIp, 68), (LOp, 69)):
-        x16 = sm(16)
+    xs = [(sm(16), out, e) for out, e in ((HIp, 68), (LOp, 69))]
+    for x16, out, e in xs:
         tt(("SM", x16[1], x16[1] + 8, 1), s0, v("V0", e, 576, 72), A.mult)
+    for x16, out, e in xs:
         tt(("SM", x16[1] + 8, x16[1] + 16, 1), s1, v("V0", e + 2, 576, 72), A.mult)
+    ms(v("ST4"), 0.0)
+    for x16, out, e in xs:
         red(out, x16)
     act(v("ZT"), v("ZB", 0, 512))
     act(v("MT"), v("ZB", 0, 512))
     for b, x in ((0, HIp), (1, LOp)):
         act(v("ZT", b, 512, 4), v("DIAG"), F.Identity, scale=x)
-    ts(Zp, HIp, 16.0, A.mult, LOp, A.add)
+    ts(v("TA"), v("TA"), BSp, A.not_equal, -BIG, A.mult)
     ts(v("OHL"), v("IREF"), LOp, A.is_equal)
-    ts(v("PA8"), PAR, 0.0, A.add)
-    spread(v("TA"), v("PA8"))
+    ts(Zp, HIp, 16.0, A.mult, LOp, A.add)
+    quant(v("W2", 384, 528), v("V1"))
     quant(v("ZQ"), v("ZT"))
     mm(PL, v("ZWQ"), v("ZQ"))
     for b, x in ((0, 16.0), (1, 1.0), (2, 128.0), (3, 1.0)):
         act(v("STT", b, 512, 4), v("OHL"), F.Identity, scale=x)
     act(v("NT"), v("ZB", 0, 512))
-    ts(v("TA"), v("TA"), PAp, A.not_equal, -BIG, A.mult)
-    ts(v("TI1"), PL, Zp, A.is_lt, TINY, A.mult)
-    tt(v("TI1"), v("TI1"), v("TA"), A.add)
     D0, D1, X0, X3, TK2 = sm(), sm(), sm(), sm(), sm()
     ts(D0, S16, HIp, A.subtract, 8.0, A.add)
     tt(D1, I16, LOp, A.subtract)
     ts(X0, BSp, S16, A.subtract, TKp, A.mult)
     ts(X3, BSp, 2.0, A.mult, TKp, A.mult)
     ts(TK2, TKp, 2.0, A.mult)
-    ts(v("M32"), v("J32"), P4, A.is_equal)
-    ts(v("JC"), J8, 16.0, A.mult, I16, A.add)
-    ms(v("ST4"), 0.0)
+    ts(v("TI1"), PL, Zp, A.is_lt, TINY, A.mult)
     ts(v("ST4", 0, 512, 4), v("QR"), Q4, A.is_equal, 4.0, A.mult)
+    ts(v("JC"), J8, 16.0, A.mult, I16, A.add)
+    tt(v("TI1"), v("TI1"), v("TA"), A.add)
     quant(v("S4Q"), v("ST4"))
 
     landed("W2", 128, hown[1], ("arr2", bcast))
@@ -457,78 +459,61 @@ def rank_program(g, core, T, topo):
         act(v("D5", b, 512, 4), v("PV", 512 * b, 512 * b + 128))
     tt(v("IND"), PS, v("THR"), A.is_gt)
     op("v", lambda: g.vector.tensor_tensor_scan(ap(v("CS")), ap(v("RM")), ap(v("IND")), 0.0, A.mult, A.add), [v("RM"), v("IND")], [v("CS")])
-    tt(v("KR1", 0, 8), v("CS", 15, 128, 16), KB, A.add)
-    pl1 = places("KR1", "KT1", "RE1", "PR1")
-    P1 = v("PR1", 0, 8)
-    t2, TG1, E1, r8, fc = sm(), sm(), sm(8), sm(8), sm()
+    for o in (0, 16):
+        tt(v("KR1", o, o + 8), v("CS", 15, 128, 16), KB, A.add)
+    pl1 = places("KR1", "KT1", "OP1")
+    t2 = sm()
     ts(t2, pl1, -1.0, A.mult, 7.0, A.add)
-    tt(TG1, pl1, t2, A.min)
-    ts(E1, P1, TG1, A.is_equal)
-    tt(r8, E1, BR, A.mult)
-    red(fc, r8)
-    ts(v("RE2"), v("Z32"), fc, A.add)
-    tr(v("FR"), v("RE2"))
-    ts(v("OFF3"), v("FR", 0, 8), 16.0, A.mult, I16, A.add)
+    scatter(v("BS"), v("B16"), v("OP1", 0, 1))
+    ts(v("TG1", 0, 1), t2, pl1, A.min)
+    gather_add(v("OFF3"), v("BS"), v("TG1", 0, 1), I16)
     landed("PH1", 0, pown[1], ("arrp", 2 * (NR - 1)))
     landed("PH1", pown[2], 128, ("arrp", 2 * (NR - 1)))
-    pick_s(v("S3"), v("PH1"), v("OFF3"))
-    pick_c(v("S3"), v("PH1"), v("OFF3"))
+    pick_s(v("S3"), v("PH1"), v("OFF3", 0, 8))
+    pick_c(v("S3"), v("PH1"), v("OFF3", 0, 8))
     bown = v("W2", 16 * me, 16 * me + 16)
     send(True, [([c], bown, v("S3", 16 * d, 16 * d + 16), 1 << engs[i], "arr3") for i, (d, c) in enumerate(zip(others, oc_))])
     send(False, [([c], v("W2s", bown[1], bown[2]), v("S3s", 16 * d, 16 * d + 16), 1 << engs[i], "arr3") for i, (d, c) in enumerate(zip(others, oc_))])
-    ts(v("OFFO", 0, 1), v("FR", me, me + 1), 16.0, A.mult, I16, A.add)
-    pick_c(bown, v("PH1"), v("OFFO", 0, 1))
-    pick_s(bown, v("PH1"), v("OFFO", 0, 1))
 
-    Mp = sm()
+    Mp, T1, PTm, fm = sm(), sm(), sm(), sm()
+    c1, c2, nw, nk, sel, G, r1, D2, Y0, D3, fl = sm(), sm(), sm(), sm(), sm(), sm(8), sm(), sm(), sm(), sm(), sm(8)
+    am = v("A1", me, me + 1)
     tt(v("CM1"), PX, v("TI1"), A.is_lt)
+    scatter(v("O1"), J16, v("OP1", 0, 1))
+    ts(v("OFFO", 0, 1), v("OFF3", me, me + 1), 0.0, A.add)
     red(Mp, v("CM1"))
+    ts(fm, v("OFF3", me, me + 1), I16, A.subtract, 0.0625, A.mult)
+    gather(v("A1"), v("O1"), v("TG1", 0, 1))
+    dma("s", ("od", 0, 1, 1), v("O1"), T.od[1:2, :], T.O1[0:1, 0:8])
     ts(v("MT", 0, 128, 4), v("M32"), Mp, A.mult, 16.0, A.min)
+    ts(T1, am, float(me), A.not_equal)
+    tt(PTm, am, fm, A.not_equal)
     quant(v("MQ"), v("MT"))
     mm(PL, v("S4Q"), v("MQ"))
-    quant(v("STQ"), v("STT"))
-    ts(v("OFFG"), v("PC", 0, 32), Q4, A.add)
-    op("v", lambda: g.vector.tensor_tensor(ap(v("VT")), ap(v("NZ1", 0, 72)).indirect(ap(v("OFFG"))), ap(v("D5")), A.add),
-       [v("NZ1", 0, 72), v("OFFG"), v("D5")], [v("VT")])
-    quant(v("W2", 256, 384), v("VT"))
-    p1m = v("PR1", me, me + 1)
-    T1, tg, em, PTm, PAm, xa, xb = sm(), sm(), sm(8), sm(), sm(), sm(8), sm(8)
-    ts(tg, p1m, -1.0, A.mult, 7.0, A.add)
-    ts(T1, p1m, 3.5, A.is_gt)
-    tt(tg, tg, p1m, A.min)
-    ts(em, P1, tg, A.is_equal)
-    tt(xa, em, TK, A.mult)
-    tt(xb, em, PAR, A.mult)
-    red(PTm, xa)
-    red(PAm, xb)
-    c1, c2, nw, nk, sel, G, r1, D2, Y0, D3 = sm(), sm(), sm(), sm(), sm(), sm(8), sm(), sm(), sm(), sm()
     tt(c1, T1, PTm, A.mult)
-    ts(r1, Mp, 15.5, A.is_lt, c1, A.mult)
+    pick_c(bown, v("PH1"), v("OFFO", 0, 1))
+    pick_s(bown, v("PH1"), v("OFFO", 0, 1))
     tt(c2, T1, c1, A.subtract)
+    ts(r1, Mp, 15.5, A.is_lt, c1, A.mult)
+    ts(v("OFFG"), v("PC", 0, 32), Q4, A.add)
     ts(nw, c2, PTm, A.add, -1.0, A.add)
     ts(Y0, X0, c2, A.mult, D0, A.add)
-    ts(D3, X3, c2, A.mult)
+    op("v", lambda: g.vector.tensor_tensor(ap(v("VT")), ap(v("NZ1", 0, 72)).indirect(ap(v("OFFG"))), ap(v("D5")), A.add),
+       [v("NZ1", 0, 72), v("OFFG"), v("D5")], [v("VT")])
     ts(nk, TKp, nw, A.mult, 1.0, A.add)
+    ts(D3, X3, c2, A.mult)
     ts(D2, TK2, c2, A.mult, r1, A.add)
-    ts(sel, PAp, PAm, A.is_equal, nk, A.mult)
+    ts(sel, BSp, fm, A.is_equal, nk, A.mult)
+    quant(v("W2", 256, 384), v("VT"))
     ts(G, J8, HIp, A.is_equal, sel, A.mult)
+    quant(v("STQ"), v("STT"))
     for b, x in enumerate((Y0, D1, D2, D3)):
         ts(v("NT", b, 32, 4), G, x, A.mult)
     quant(v("NTQ"), v("NT"))
     mm(v("PD", 0, 128), v("STQ"), v("NTQ"))
-    fl = sm(8)
+    quant(v("WQ"), v("WT"))
     tt(fl, v("PD", 0, 8), v("JC"), A.add)
     cp(v("OFFF"), fl)
-    quant(v("WQ"), v("WT"))
-    for t, pr in ((0, PR), (1, P1)):
-        x8, xc = sm(8), sm()
-        ts(x8, pr, Q32, A.is_equal)
-        tt(x8, x8, J8, A.mult)
-        red(xc, x8)
-        ts(v("RO%d" % t), v("Z32"), xc, A.add)
-        tr(v("OD%d" % t), v("RO%d" % t))
-        o = v("OD%d" % t)[1]
-        dma("s", ("od", 0, 1, 1), v("OD%d" % t), T.od[t:t + 1, :], T.R32[0:1, o:o + 8])
 
     landed("W2", 0, bown[1], ("arr3", 2 * (NR - 1)))
     landed("W2", bown[2], 128, ("arr3", 2 * (NR - 1)))

from concourse.bass import DstId, RemoteDMATransfer
from concourse.mybir import dt, AluOpType, AxisListType, ActivationFunctionType

A = AluOpType
F = ActivationFunctionType
NR, SL = 8, 18
ROWS = {"KR": 32, "KT": 32, "KR1": 32, "KT1": 32, "FS": 16, "FBR": 16, "BR": 16, "B16": 16, "BS": 16, "A1": 16, "F16": 16, "J18": 16}
RN = list(ROWS)
TINY, BIG = 2.0 ** -100, 1e29

_f, _b, _u = "float32", "bfloat16", "uint16"


def _mx(d, name, n):
    d[name] = ("sbuf", [128, n], "float8_e4m3fn_x4")
    d[name + "s"] = ("sbuf", [128, n], "uint8")


SCRATCH = {}
for _n, _w, _t in (
        ("TB", 512, _b), ("UC", 4, _b), ("NUC", 4, _b), ("NZ", 128, _b), ("WT", 512, _b), ("ZB", 576, _b), ("UT", 512, _b), ("NU", 512, _b),
        ("CI", 8, "int32"), ("CF", 8, _f), ("CK", 16, _f), ("J32", 32, _f), ("KI", 128, _b), ("IREF", 128, _b), ("OH2", 256, _b),
        ("OHREF", 512, _b), ("QR", 128, _b), ("ZE", 520, _b), ("TIE", 128, _f), ("DIAG", 128, _f), ("RM", 128, _f),
        ("M32", 32, _f), ("MS", 8, _f), ("JC", 8, _f), ("TIE8", 8, _f), ("WN", 32, _f), ("O0", 16, _f), ("O1", 16, _f),
        ("MVC", 512, _b), ("ONE", 512, _b), ("ZW", 512, _b), ("ST4", 512, _b), ("NT0", 576, _b), ("NT1", 576, _b),
        ("INFO", 512, _b), ("OHT", 512, _b), ("CMP", 128, _f), ("SM", 384, _f), ("R32", 32 * len(ROWS), _f),
        ("V0", 576, _b), ("V1", 576, _b), ("NZ1", 80, _f), ("TH8", 8, _f), ("THR", 128, _f), ("ZT", 512, _b),
        ("TI1", 128, _f), ("TA", 128, _f), ("IND", 128, _f), ("CS", 128, _f),
        ("D5", 512, _f), ("MT", 512, _b), ("VT", 512, _b), ("OHL", 128, _b), ("STT", 512, _b), ("NT", 512, _b), ("Y", 128, _f), ("CM1", 128, _f),
        ("OFF1", 4, _u), ("OFFH", 18, _u), ("OFF3", 16, _u), ("OP0", 2, _u), ("OP1", 2, _u), ("OX0", 2, _u), ("TG0", 2, _u), ("TG1", 2, _u),
        ("OFFO", 2, _u), ("OFFG", 32, _u), ("OFFF", 8, _u), ("OFT", 8, _u)):
    SCRATCH[_n] = ("sbuf", [128, _w], _t)
for _n, _w in (("UQ", 128), ("NUQ", 128), ("TQ", 128), ("MVQ", 128), ("OHQ", 128), ("ONQ", 128), ("EQ", 512), ("N0Q", 144), ("N1Q", 144),
               ("WQ", 128), ("ZWQ", 128), ("S4Q", 128), ("L1S", 144), ("LD1", 144), ("NB", 160), ("W2", 528), ("PH1", 128), ("S3", 128),
               ("ZQ", 128), ("MQ", 128), ("STQ", 128), ("NTQ", 128), ("FT", 128), ("HT", 128)):
    _mx(SCRATCH, _n, _w)
for _n, _w in (("PV", 2048), ("PA", 512), ("PB", 512), ("PC", 512), ("PD", 512)):
    SCRATCH[_n] = ("psum", [128, _w], _f)

SEMAPHORES = ["sv", "sa", "st", "sg", "arrh", "arrg", "arr1", "arr2", "arr3", "arrp"]
SEMAPHORES += ["d%d" % i for i in range(24)] + ["l%d" % i for i in range(12)]


def _helper_of(topo, core):
    return [c for c in topo.cores_of(core) if topo.die(c) != topo.die(core)][0]


def _dst(topo, d, s):
    rid, pid = topo.addr(d, s)
    return DstId(rid=rid, pnc=pid)


def _hand_on(g, core, T, topo, owner):
    me = T.rank_of(owner)
    near, far = topo.engines(owner, core), len(topo.engines(owner, T.cores[me - 1]))
    for k, (src, dst, sem, n) in enumerate((("HT", "PH1", "arrh", len(near)), ("HTs", "PH1s", "arrg", len(near) - far))):
        g.wait_ge(T.sem[sem], n)
        tr = []
        for i, d in enumerate((me + x) % NR for x in range(1, NR)):
            c = T.cores[d]
            s, t = T[src][:, 16 * d:16 * d + 16], T[dst][:, 16 * me:16 * me + 16]
            if k == 0:
                s, t = s.bitcast(dt.uint8), t.bitcast(dt.uint8)
            tr.append(RemoteDMATransfer(dst_ids=[_dst(topo, c, core)], dma_engine_mask=1 << topo.engines(core, c)[i],
                                        remote_sem=T.sem.arrp, srcs=[s], dsts=[t]))
        g.remote_dma_fused(tr, local_sem=T.sem["l%d" % k])
    for k in range(2):
        g.wait_ge(T.sem["l%d" % k], NR - 1)


def rank_program(g, core, T, topo):
    me = T.rank_of(core)
    if me is None:
        for c in T.cores:
            if _helper_of(topo, c) == core:
                _hand_on(g, core, T, topo, c)
        return
    ENG = {"v": g.vector, "a": g.scalar, "t": g.tensor, "g": g, "s": g.sync}
    SEM = {"v": "sv", "a": "sa", "t": "st", "g": "sg"}
    cnt, seen, acc, nd, nl, ends = {}, {q: {} for q in ENG}, {}, [0], [0], []

    def clash(a, lo, hi, st):
        if a[1] <= lo or hi <= a[0]:
            return False
        return not (a[2] == st and st > 1 and a[0] % st != lo % st)

    def span(x):
        if SCRATCH[x[0]][0] == "psum":
            return x[0], x[1] // 512 * 512, (x[2] + 511) // 512 * 512, 1
        return x[0], x[1], x[2], x[3]

    def waits(q, rd, wr, dma=False):
        need = {}
        for w, xs in ((False, rd), (True, wr)):
            for x in xs:
                if x[0] not in SCRATCH:
                    continue
                n, lo, hi, st = span(x)
                ps = SCRATCH[n][0] == "psum"
                for a in acc.get(n, []):
                    if not clash(a, lo, hi, st):
                        continue
                    same = a[4] == q and not dma and not a[6]
                    if same and (q == "t" or not a[3]):
                        continue
                    if not (w or a[3]) and (same or not ps):
                        continue
                    need[a[5][0]] = max(need.get(a[5][0], 0), a[5][1])
        for s, val in need.items():
            if seen[q].get(s, 0) < val:
                ENG[q].wait_ge(T.sem[s], val)
                seen[q][s] = val

    def note(q, rd, wr, tok, dma=False):
        for w, xs in ((False, rd), (True, wr)):
            for x in xs:
                if x[0] in SCRATCH:
                    n, lo, hi, st = span(x)
                    acc.setdefault(n, []).append((lo, hi, st, w, q, tok, dma))

    def v(n, lo=0, hi=None, st=1):
        if n in ROWS:
            o = 32 * RN.index(n)
            return ("R32", o + lo, o + (ROWS[n] if hi is None else hi), st)
        return (n, lo, SCRATCH[n][1][1] if hi is None else hi, st)

    def ap(x):
        return T[x[0]][:, x[1]:x[2]] if x[3] == 1 else T[x[0]][:, x[1]:x[2]:x[3]]

    def op(q, fn, rd, wr):
        waits(q, rd, wr)
        cnt[q] = cnt.get(q, 0) + 1
        fn().then_inc(T.sem[SEM[q]], 1)
        note(q, rd, wr, (SEM[q], cnt[q]))

    def sc(x):
        return ap(x) if isinstance(x, tuple) else x

    def ts(out, in0, s1, op0, s2=None, op1=None):
        rd = [in0] + [s for s in (s1, s2) if isinstance(s, tuple)]
        if op1 is None:
            op("v", lambda: g.vector.tensor_scalar(ap(out), ap(in0), sc(s1), None, op0), rd, [out])
        else:
            op("v", lambda: g.vector.tensor_scalar(ap(out), ap(in0), sc(s1), sc(s2), op0, op1), rd, [out])

    def tt(out, a, b, o):
        op("v", lambda: g.vector.tensor_tensor(ap(out), ap(a), ap(b), o), [a, b], [out])

    def red(out, a):
        op("v", lambda: g.vector.tensor_reduce(ap(out), ap(a), AxisListType.X, A.add), [a], [out])

    def cp(out, a):
        op("v", lambda: g.vector.tensor_copy(ap(out), ap(a)), [a], [out])

    def tr(out, a):
        op("v", lambda: g.vector.transpose(ap(out), ap(a)), [a], [out])

    def ms(out, c):
        op("v", lambda: g.vector.memset(ap(out), c), [], [out])

    def act(out, a, fn=F.Copy, **kw):
        k2 = {k: sc(x) for k, x in kw.items()}
        op("a", lambda: g.scalar.activation(ap(out), ap(a), fn, **k2), [a] + [x for x in kw.values() if isinstance(x, tuple)], [out])

    def quant(out, in_):
        o2 = v(out[0] + "s", out[1], out[2])
        op("v", lambda: g.vector.quantize_mx(ap(out), ap(o2), ap(in_)), [in_], [out, o2])

    def mm(out, w, x, start=True, stop=True):
        ws, xs = v(w[0] + "s", w[1], w[2]), v(x[0] + "s", x[1], x[2])
        op("t", lambda: g.tensor.matmul_mx(ap(out), ap(w), ap(ws), ap(x), ap(xs), start, stop), [w, ws, x, xs], [out])

    def scatter(out, in_, off):
        op("v", lambda: g.vector.tensor_copy(ap(out).indirect(ap(off)), ap(in_)), [in_, off], [out])

    def gather(out, win, off):
        op("v", lambda: g.vector.tensor_copy(ap(out), ap(win).indirect(ap(off))), [win, off], [out])

    def gather_add(out, win, off, col):
        op("v", lambda: g.vector.tensor_scalar(ap(out), ap(win).indirect(ap(off)), ap(col), None, A.add), [win, off, col], [out])

    def pick_c(out, win, off):
        op("v", lambda: g.vector.tensor_copy(ap(out).bitcast(dt.uint32), ap(win).bitcast(dt.uint32).indirect(ap(off))), [win, off], [out])

    def pick_s(out, win, off):
        out, win = v(out[0] + "s", out[1], out[2]), v(win[0] + "s", win[1], win[2])
        op("a", lambda: g.scalar.activation(ap(out), ap(win).indirect(ap(off)), F.Copy), [win, off], [out])

    def dma(q, out, in_, oap=None, iap=None):
        waits(q, [in_], [out], True)
        s = "d%d" % nd[0]
        nd[0] += 1
        ENG[q].dma_start(ap(out) if oap is None else oap, ap(in_) if iap is None else iap).then_inc(T.sem[s], 16)
        note(q, [in_], [out], (s, 16), True)
        ends.append((s, 16))

    def codes(x):
        return ap(x).bitcast(dt.uint8)

    def landed(n, lo, hi, tok):
        if hi > lo:
            for m in (n, n + "s"):
                note("-", [], [v(m, lo, hi)], tok, True)

    def send(x, transfers):
        waits("g", [t[2] for t in transfers], [], True)
        s, n = "l%d" % nl[0], 0
        nl[0] += 1
        out = []
        for dc, y, z, mask, sem in transfers:
            cast = codes if x else ap
            out.append(RemoteDMATransfer(dst_ids=[_dst(topo, c, core) for c in dc], dma_engine_mask=mask, remote_sem=T.sem[sem],
                                         srcs=[cast(z)], dsts=[cast(y) for c in dc]))
            n += bin(mask).count("1")
        g.remote_dma_fused(out, local_sem=T.sem[s])
        note("g", [t[2] for t in transfers], [], (s, n), True)
        ends.append((s, n))

    others = [(me + i) % NR for i in range(1, NR)]
    oc_ = [T.cores[d] for d in others]
    helper = _helper_of(topo, core)
    engs = topo.engines(core, oc_[0])
    m_all = topo.mask(core, oc_[0])
    m_help = topo.mask(core, helper)
    m_far = m_help & ~m_all
    bcast = 2 * len(engs) * (NR - 1)

    smn = [0]

    def sm(n=1):
        smn[0] += n
        return ("SM", smn[0] - n, smn[0], 1)

    dma("s", v("TB"), v("TB"), None, T.tb[:, :])
    dma("a", v("UC"), v("UC"), None, T.u[:, 0:4])
    dma("a", v("NZ"), v("NZ"), None, T.nz[:, :])
    dma("s", v("WT"), v("WT"), None, T.w[:, :])

    def iota(out, pattern, mult, small=True, base=0):
        if small:
            op("g", lambda: g.iota(ap(out), pattern, base, mult, allow_small_or_imprecise_dtypes=True), [], [out])
        else:
            op("g", lambda: g.iota(ap(out), pattern, base, mult), [], [out])

    iota(v("CI", 0, 1), [[0, 1]], 1, False)
    iota(v("KI"), [[1, 128]], 0)
    iota(v("OH2"), [[0, 8], [1, 16], [16, 2]], 0)
    iota(v("J32"), [[1, 32]], 0)
    iota(v("IREF"), [[0, 8], [1, 16]], 0)

    ms(v("ZB"), 0.0)
    act(v("MVC"), v("ZB", 0, 512))
    ci, cf, ck = (lambda i: v("CI", i, i + 1)), (lambda i: v("CF", i, i + 1)), (lambda i: v("CK", i, i + 1))
    J8, J16 = v("J32", 0, 8), v("J32", 0, 16)
    ts(ci(1), ci(0), 15, A.bitwise_and)
    ts(ci(2), ci(0), 4, A.logical_shift_right)
    ts(ci(4), ci(0), 3, A.bitwise_and)
    ts(ci(5), ci(0), 2, A.logical_shift_right)
    ts(ci(3), ci(0), 31, A.bitwise_and)
    cp(v("CF", 0, 6), v("CI", 0, 6))
    P, I16, S16, Q4, P4 = cf(0), cf(1), cf(2), cf(4), cf(5)
    ts(v("TIE"), v("KI"), P, A.is_lt, TINY, A.mult)
    for h in range(2):
        act(v("OHREF", h, 512, 2), v("OH2"))
    ts(ck(1), S16, 16.0, A.mult)
    for e, x in ((0, ck(1)), (1, I16), (10, ck(1)), (11, I16), (16, S16), (21, I16), (26, S16), (31, I16)):
        act(v("MVC", e, e + 1), x)

    ts(v("NUC"), v("UC"), -1.0, A.mult)
    for b in range(4):
        ts(v("UT", b, 512, 4), v("ZB", 0, 128), v("UC", b, b + 1), A.add)
        act(v("NU", b, 512, 4), v("ZB", 0, 128), F.Identity, bias=v("NUC", b, b + 1))
    act(v("INFO"), v("ZB", 0, 512))
    act(v("ZE"), v("ZB", 0, 520))

    TQ = v("TQ")
    quant(TQ, v("TB"))
    send(True, [([helper], v("HT"), TQ, m_help, "arrh")])
    quant(v("UQ"), v("UT"))
    quant(v("NUQ"), v("NU"))
    PX, PS, PL, PF = v("PA", 0, 128), v("PB", 0, 128), v("PC", 0, 128), v("PD", 0, 144)
    mm(PX, v("UQ"), TQ, True, False)
    mm(PX, TQ, v("NUQ"), False, True)
    mm(PS, TQ, v("UQ"))
    quant(v("MVQ"), v("MVC"))
    rk = sm()
    tt(v("CMP"), PX, v("TIE"), A.is_lt)
    red(rk, v("CMP"))
    ts(v("OHT"), v("OHREF"), rk, A.is_equal)
    quant(v("OHQ"), v("OHT"))
    ts(v("INFO", 0, 1), v("PB", 0, 1), 0.0, A.is_gt)
    mm(PL, v("OHQ"), v("MVQ"))
    cp(v("OFF1"), v("PC", 0, 4))
    cp(v("INFO", 4, 8), v("PC", 4, 8))
    pick_s(v("L1S", 0, 16), TQ, v("OFF1", 0, 1))
    pick_c(v("L1S", 0, 16), TQ, v("OFF1", 0, 1))
    quant(v("L1S", 16, 144), v("INFO"))
    own = v("LD1", SL * me, SL * me + SL)
    send(True, [(oc_, own, v("L1S", 0, SL), m_all, "arr1")])
    send(False, [(oc_, v("LD1s", own[1], own[2]), v("L1Ss", 0, SL), m_all, "arr1")])
    send(False, [([helper], v("HTs"), v("TQs"), m_far, "arrg")])
    dma("s", own, v("L1S", 0, SL), codes(own), codes(v("L1S", 0, SL)))
    dma("s", v("LD1s", own[1], own[2]), v("L1Ss", 0, SL))
    pown = v("PH1", 16 * me, 16 * me + 16)
    town = v("TQ", 16 * me, 16 * me + 16)
    dma("s", pown, town, codes(pown), codes(town))
    dma("s", v("PH1s", pown[1], pown[2]), v("TQs", town[1], town[2]))
    pick_s(v("NB", 144, 160), TQ, v("OFF1", 2, 3))
    pick_c(v("NB", 144, 160), TQ, v("OFF1", 2, 3))

    for n in ("KR", "KR1"):
        iota(v(n), [[0, 2], [-1, 16]], 0, True, 7)
    iota(v("QR"), [[0, 8], [1, 4], [0, 4]], 0)
    ts(v("ZE", 4, 516, 4), v("KI"), P, A.is_equal, 0.5, A.mult)
    ts(v("TIE8"), J8, -0.125, A.mult, 0.875, A.add)
    for b in range(4):
        quant(v("EQ", 128 * b, 128 * b + 128), v("ZE", 4 - b, 516 - b))
    E = [v("EQ", 128 * b, 128 * b + 128) for b in range(4)]
    for t in (0, 1):
        n = "NT%d" % t
        act(v(n), v("ZB"))
        for a in range(NR):
            act(v(n, 72 * a, 72 * a + 64), v("NZ", 64 * t, 64 * t + 64))
        quant(v("N%dQ" % t), v(n))
        if t == 0:
            act(v("ONE"), v("ZB", 0, 512))
            ms(v("ONE", 0, 512, 4), 1.0)
            ts(v("J18"), J16, float(SL), A.mult)
            ms(v("WN", 16, 32), float(SL * NR))
            quant(v("ONQ"), v("ONE"))
    PVb = [v("PV", 512 * b, 512 * b + 144) for b in range(4)]
    for b in range(4):
        mm(PVb[b], E[b], v("N1Q"))
    ms(v("NZ1", 64, 80), 0.0)
    for b in range(4):
        act(v("NZ1", b, 64, 4), v("PV", 512 * b, 512 * b + 16))
    for b in range(4):
        mm(PVb[b], E[b], v("N0Q"), True, False)
    ms(v("F16"), 0.0)
    ts(v("OFT"), J8, 0.0, A.add)
    ts(v("RM"), v("IREF"), 0.0, A.is_gt)
    ts(v("MS"), J8, S16, A.is_equal)
    ms(v("ZW"), 0.0)
    ts(v("DIAG"), v("KI"), P, A.is_equal)
    for b, x in ((0, 16.0), (1, 1.0)):
        ms(v("ZW", b, 512, 4), x)
    quant(v("ZWQ"), v("ZW"))

    landed("LD1", 0, own[1], ("arr1", bcast))
    landed("LD1", own[2], 144, ("arr1", bcast))
    mm(PF, v("ONQ"), v("LD1"))
    for b in range(4):
        mm(PVb[b], E[b], v("LD1"), False, True)
    for b in range(4):
        act(v("V0", b, 576, 4), PVb[b])
    FIT = v("PD", 16, 144, SL)

    def places(kr, kt, off):
        pl, c16 = sm(), sm(16)
        tr(v(kt), v(kr))
        ts(c16, v(kr, 0, 16), v(kt, 0, 1), A.is_gt)
        red(pl, c16)
        ts(v(off, 0, 1), pl, 0.0, A.add)
        return pl

    for o in (0, 16):
        tt(v("KR", o, o + 8), FIT, v("TIE8"), A.add)
    pl0 = places("KR", "KT", "OP0")
    gv = sm()
    ts(gv, pl0, 3.5, A.is_lt, 16.0, A.mult)
    scatter(v("WN", 0, 16), v("J18"), v("OP0", 0, 1))
    ts(v("OX0", 0, 1), gv, pl0, A.subtract, 7.0, A.add)
    sh = me % 2
    gather_add(v("OFFH", sh, sh + 16), v("WN"), v("OX0", 0, 1), I16)
    oh = v("OFFH", me + sh, me + sh + 1)
    quant(v("NB", 0, 144), v("V0"))
    hown = v("W2", 128 + 16 * me, 144 + 16 * me)
    pick_c(hown, v("NB"), oh)
    pick_s(hown, v("NB"), oh)
    hos = v("W2s", hown[1], hown[2])
    send(True, [(oc_, hown, hown, m_all, "arr2")])
    send(False, [(oc_, hos, hos, m_all, "arr2")])

    for b in range(4):
        mm(PVb[b], E[b], v("N1Q"), True, False)
        mm(PVb[b], E[b], v("LD1"), False, True)
    for b in range(4):
        act(v("V1", b, 576, 4), PVb[b])
    TK, t1, CAP, KB = sm(8), sm(), sm(8), sm(8)
    ts(t1, pl0, -1.0, A.mult, 7.0, A.add)
    cp(v("F16", 0, 8), FIT)
    scatter(v("O0"), J16, v("OP0", 0, 1))
    ts(v("TG0", 0, 1), t1, pl0, A.min)
    scatter(v("FS"), v("F16"), v("OP0", 0, 1))
    gather(v("BR"), v("O0"), v("TG0", 0, 1))
    gather(v("FBR"), v("FS"), v("TG0", 0, 1))
    BR = v("BR", 0, 8)
    dma("s", ("od", 0, 1, 1), v("O0"), T.od[0:1, :], T.O0[0:1, 0:8])
    TKp, BSp, HIp, LOp, Zp, xa, xb = sm(), sm(), sm(), sm(), sm(), sm(8), sm(8)
    tt(TK, BR, J8, A.not_equal)
    tt(xb, BR, v("MS"), A.mult)
    ts(v("B16"), v("BR"), 16.0, A.mult)
    ts(v("TH8"), TK, -BIG, A.mult, BIG, A.add)
    ts(CAP, TK, -1000.0, A.mult, 1112.0, A.add)
    tt(xa, TK, v("MS"), A.mult)
    red(BSp, xb)
    gather(v("THR"), v("TH8"), v("OFT"))
    tt(CAP, v("FBR", 0, 8), CAP, A.min)
    red(TKp, xa)
    sl, s0, s1 = sm(8), sm(8), sm(8)
    ts(sl, J8, BSp, A.is_equal, 2.0, A.mult)
    tt(KB, CAP, v("TIE8"), A.add)
    ts(v("M32"), v("J32"), P4, A.is_equal)
    ts(s0, sl, TKp, A.mult)
    gather(v("TA"), BR, v("OFT"))
    tt(s1, sl, s0, A.subtract)
    xs = [(sm(16), out, e) for out, e in ((HIp, 68), (LOp, 69))]
    for x16, out, e in xs:
        tt(("SM", x16[1], x16[1] + 8, 1), s0, v("V0", e, 576, 72), A.mult)
    for x16, out, e in xs:
        tt(("SM", x16[1] + 8, x16[1] + 16, 1), s1, v("V0", e + 2, 576, 72), A.mult)
    ms(v("ST4"), 0.0)
    for x16, out, e in xs:
        red(out, x16)
    act(v("ZT"), v("ZB", 0, 512))
    act(v("MT"), v("ZB", 0, 512))
    for b, x in ((0, HIp), (1, LOp)):
        act(v("ZT", b, 512, 4), v("DIAG"), F.Identity, scale=x)
    ts(v("TA"), v("TA"), BSp, A.not_equal, -BIG, A.mult)
    ts(v("OHL"), v("IREF"), LOp, A.is_equal)
    ts(Zp, HIp, 16.0, A.mult, LOp, A.add)
    quant(v("W2", 384, 528), v("V1"))
    quant(v("ZQ"), v("ZT"))
    mm(PL, v("ZWQ"), v("ZQ"))
    for b, x in ((0, 16.0), (1, 1.0), (2, 128.0), (3, 1.0)):
        act(v("STT", b, 512, 4), v("OHL"), F.Identity, scale=x)
    act(v("NT"), v("ZB", 0, 512))
    D0, D1, X0, X3, TK2 = sm(), sm(), sm(), sm(), sm()
    ts(D0, S16, HIp, A.subtract, 8.0, A.add)
    tt(D1, I16, LOp, A.subtract)
    ts(X0, BSp, S16, A.subtract, TKp, A.mult)
    ts(X3, BSp, 2.0, A.mult, TKp, A.mult)
    ts(TK2, TKp, 2.0, A.mult)
    ts(v("TI1"), PL, Zp, A.is_lt, TINY, A.mult)
    ts(v("ST4", 0, 512, 4), v("QR"), Q4, A.is_equal, 4.0, A.mult)
    ts(v("JC"), J8, 16.0, A.mult, I16, A.add)
    tt(v("TI1"), v("TI1"), v("TA"), A.add)
    quant(v("S4Q"), v("ST4"))

    landed("W2", 128, hown[1], ("arr2", bcast))
    landed("W2", hown[2], 256, ("arr2", bcast))
    H = v("W2", 128, 256)
    mm(PS, v("UQ"), H)
    mm(PX, v("UQ"), H, True, False)
    mm(PX, H, v("NUQ"), False, True)
    for b in range(4):
        mm(v("PV", 512 * b, 512 * b + 128), E[b], H)
    for b in range(4):
        act(v("D5", b, 512, 4), v("PV", 512 * b, 512 * b + 128))
    tt(v("IND"), PS, v("THR"), A.is_gt)
    op("v", lambda: g.vector.tensor_tensor_scan(ap(v("CS")), ap(v("RM")), ap(v("IND")), 0.0, A.mult, A.add), [v("RM"), v("IND")], [v("CS")])
    for o in (0, 16):
        tt(v("KR1", o, o + 8), v("CS", 15, 128, 16), KB, A.add)
    pl1 = places("KR1", "KT1", "OP1")
    t2 = sm()
    ts(t2, pl1, -1.0, A.mult, 7.0, A.add)
    scatter(v("BS"), v("B16"), v("OP1", 0, 1))
    ts(v("TG1", 0, 1), t2, pl1, A.min)
    gather_add(v("OFF3"), v("BS"), v("TG1", 0, 1), I16)
    landed("PH1", 0, pown[1], ("arrp", 2 * (NR - 1)))
    landed("PH1", pown[2], 128, ("arrp", 2 * (NR - 1)))
    pick_s(v("S3"), v("PH1"), v("OFF3", 0, 8))
    pick_c(v("S3"), v("PH1"), v("OFF3", 0, 8))
    bown = v("W2", 16 * me, 16 * me + 16)
    send(True, [([c], bown, v("S3", 16 * d, 16 * d + 16), 1 << engs[i], "arr3") for i, (d, c) in enumerate(zip(others, oc_))])
    send(False, [([c], v("W2s", bown[1], bown[2]), v("S3s", 16 * d, 16 * d + 16), 1 << engs[i], "arr3") for i, (d, c) in enumerate(zip(others, oc_))])

    Mp, T1, PTm, fm = sm(), sm(), sm(), sm()
    c1, c2, nw, nk, sel, G, r1, D2, Y0, D3, fl = sm(), sm(), sm(), sm(), sm(), sm(8), sm(), sm(), sm(), sm(), sm(8)
    am = v("A1", me, me + 1)
    tt(v("CM1"), PX, v("TI1"), A.is_lt)
    scatter(v("O1"), J16, v("OP1", 0, 1))
    ts(v("OFFO", 0, 1), v("OFF3", me, me + 1), 0.0, A.add)
    red(Mp, v("CM1"))
    ts(fm, v("OFF3", me, me + 1), I16, A.subtract, 0.0625, A.mult)
    gather(v("A1"), v("O1"), v("TG1", 0, 1))
    dma("s", ("od", 0, 1, 1), v("O1"), T.od[1:2, :], T.O1[0:1, 0:8])
    ts(v("MT", 0, 128, 4), v("M32"), Mp, A.mult, 16.0, A.min)
    ts(T1, am, float(me), A.not_equal)
    tt(PTm, am, fm, A.not_equal)
    quant(v("MQ"), v("MT"))
    mm(PL, v("S4Q"), v("MQ"))
    tt(c1, T1, PTm, A.mult)
    pick_c(bown, v("PH1"), v("OFFO", 0, 1))
    pick_s(bown, v("PH1"), v("OFFO", 0, 1))
    tt(c2, T1, c1, A.subtract)
    ts(r1, Mp, 15.5, A.is_lt, c1, A.mult)
    ts(v("OFFG"), v("PC", 0, 32), Q4, A.add)
    ts(nw, c2, PTm, A.add, -1.0, A.add)
    ts(Y0, X0, c2, A.mult, D0, A.add)
    op("v", lambda: g.vector.tensor_tensor(ap(v("VT")), ap(v("NZ1", 0, 72)).indirect(ap(v("OFFG"))), ap(v("D5")), A.add),
       [v("NZ1", 0, 72), v("OFFG"), v("D5")], [v("VT")])
    ts(nk, TKp, nw, A.mult, 1.0, A.add)
    ts(D3, X3, c2, A.mult)
    ts(D2, TK2, c2, A.mult, r1, A.add)
    ts(sel, BSp, fm, A.is_equal, nk, A.mult)
    quant(v("W2", 256, 384), v("VT"))
    ts(G, J8, HIp, A.is_equal, sel, A.mult)
    quant(v("STQ"), v("STT"))
    for b, x in enumerate((Y0, D1, D2, D3)):
        ts(v("NT", b, 32, 4), G, x, A.mult)
    quant(v("NTQ"), v("NT"))
    mm(v("PD", 0, 128), v("STQ"), v("NTQ"))
    quant(v("WQ"), v("WT"))
    tt(fl, v("PD", 0, 8), v("JC"), A.add)
    cp(v("OFFF"), fl)

    landed("W2", 0, bown[1], ("arr3", 2 * (NR - 1)))
    landed("W2", bown[2], 128, ("arr3", 2 * (NR - 1)))
    pick_c(v("FT"), v("W2"), v("OFFF"))
    pick_s(v("FT"), v("W2"), v("OFFF"))
    dma("s", ("oc", 0, 1, 1), v("FT"), T.oc[:, :], codes(v("FT")))
    mm(PS, v("WQ"), v("FT"))
    for k in range(4):
        dma("a", ("osc", 0, 1, 1), v("FTs"), T.osc[4 * k:4 * k + 4, :], T.FTs[32 * k:32 * k + 4, 0:128])
    cp(v("Y"), PS)
    dma("s", ("y", 0, 1, 1), v("Y"), T.y[:, :])

    for q in ("v", "a", "t", "g"):
        g.wait_ge(T.sem[SEM[q]], cnt[q])
    for s, n in ends:
        g.wait_ge(T.sem[s], n)
